import numpy as np, ml_dtypes
CORES = [51,54,179,182]
N = 4
BF = ml_dtypes.bfloat16
def gentries(a):
    return np.ascontiguousarray(a.reshape(8, 16, -1).transpose(0, 2, 1)).reshape(8, -1)
def gtable(e):
    e = np.asarray(e); return np.ascontiguousarray(e.reshape(8, -1, 16).transpose(0, 2, 1)).reshape(128, -1).astype(np.int32)
V, P, T, TL, Q, M = 1792, 256, 9, 3, 10, 2048
def money(rng, base):
    v = base + rng.integers(-3, 4, base.shape[:2] + (16, base.shape[-1]))
    return np.clip(np.floor(v), 0, 15).astype(np.int64)
def parts(rng):
    x = money(rng, 16 * rng.random((N, 8, 1, V)) ** rng.choice(np.array([2.0, 3.0, 5.0]), (N, 8, 1, 1)))
    price = money(rng, 16 * rng.random((N, 8, 1, P)))
    pool = rng.integers(0, V, (N, 8, 64))
    pop = np.take_along_axis(pool, rng.integers(0, 64, (N, 8, 16 * V)), 2).reshape(N, 8, 16, V)
    kin = np.where(rng.random((N, 8, 16, V)) < 0.15, pop, rng.integers(0, V, (N, 8, 16, V)))
    few = np.take_along_axis(pool, rng.integers(0, 48, (N, 8, P)), 2)
    own = np.where(rng.random((N, 8, P)) < 0.5, few, rng.integers(0, V, (N, 8, P)))
    hold = rng.integers(0, V, (N, 8, P)); wall = rng.integers(0, 2, (N, 8, P)); wt = rng.integers(0, 256, (N, 8, 16))
    return x, kin, own, hold, wall, price, wt
def pack(x, kin, own, hold, wall, price, wt):
    return {"x": np.ascontiguousarray(x.reshape(N, 128, V)).astype(np.float32).astype(BF), "kin": np.ascontiguousarray(kin.reshape(N, 128, V)).astype(np.int32),
            "own": np.stack([gtable(a) for a in own]), "hold": np.stack([gtable(a) for a in hold]), "wall": np.stack([gtable(a) for a in wall]),
            "price": np.ascontiguousarray(price.reshape(N, 128, P)).astype(np.float32).astype(BF), "wt": np.ascontiguousarray(wt.reshape(N, 128, 1)).astype(np.int32)}
def setup_inputs(rng):
    return pack(*parts(rng))
def setup_inputs_alike(rng):
    x, kin, own, hold, wall, price, wt = parts(rng)
    kin[:, 0] = kin[:, 0, :, :1].copy()
    kin[:, 1] = kin[:, 1, :1, :].copy()
    own[:, 2] = own[:, 2, :1].copy()
    kin[:, 3] = rng.integers(0, V, (N, 1, 1))
    own[:, 4] = np.take_along_axis(rng.integers(0, V, (N, 3)), rng.integers(0, 3, (N, P)), 1)
    own[:, 5] = np.argsort(rng.random((N, V)), axis=-1)[:, :P]; price[:, 5] = 15; x[:, 5] = 0; x[:, 5, 3] = rng.integers(0, 2, (N, V))
    own[1::2, 5, P - 1] = own[1::2, 5, 0]; price[1::2, 5, 3, P - 1] = 0
    x[:, 6] = x[:, 6, :, :1].copy(); hold[:, 6] = hold[:, 6, :1].copy()
    kin[:, 7] = rng.choice(np.array([0, 1, V - 2, V - 1]), (N, 16, V)); own[:, 7] = rng.choice(np.array([0, V - 1]), (N, P))
    return pack(x, kin, own, hold, wall, price, wt)
def setup_inputs_corners(rng):
    x, kin, own, hold, wall, price, wt = parts(rng); q = rng.permutation(8); a = np.arange(V)
    for r in range(N):
        g = q[0]; x[r, g] = 0; price[r, g] = 15; kin[r, g] = np.minimum(a + 1, V - 1); own[r, g, ::8] = V - 1; own[r, g, 1::8] = 0; own[r, g, 2::8] = V - 2
        g = q[1]; kin[r, g] = a; own[r, g, :2] = 0; own[r, g, P - 2:] = V - 1
        g = q[2]; price[r, g] = 0; wt[r, g] = 255 * (r % 2)
        g = q[3]; x[r, g] = 15; price[r, g] = 15; wt[r, g] = 255; wall[r, g] = 1; hold[r, g, ::2] = V - 1; hold[r, g, 1::4] = 0
        kin[r, g, 0] = rng.permutation(V); own[r, g] = rng.permutation(V)[:P]
        if r % 2 == 1: own[r, g, P - 1] = own[r, g, 0]; price[r, g, :, P - 1] = 7
        g = q[4 + r % 4]; kin[r, g] = rng.integers(0, 2, (16, V)) * (V - 1); own[r, g] = rng.integers(0, 2, P) * (V - 1)
        g = q[4 + (r + 1) % 4]; wall[r, g] = 0; wt[r, g] = 0
        g = q[4 + (r + 2) % 4]; x[r, g] = 0; x[r, g, :, 0] = 15; price[r, g] = 15; kin[r, g] = np.maximum(a - 1, 0); own[r, g] = rng.integers(0, 2 * T, P)
        g = q[4 + (r + 3) % 4]; wall[r, g] = 1; hold[r, g] = rng.integers(0, 2, P) * (V - 1); kin[r, g, :, V - 1] = 0; kin[r, g, :, 0] = V - 1
    return pack(x, kin, own, hold, wall, price, wt)
def setup_inputs_ends(rng):
    def rec(n):
        k = rng.random((N, 8, 1, n)); el = rng.integers(0, 2, (N, 8, 16, n))
        return 15 * np.where(k < 0.35, 0, np.where(k < 0.7, 1, el))
    x = rec(V); price = rec(P)
    kin = np.where(rng.random((N, 8, 1, V)) < 0.7, rng.integers(0, 2, (N, 8, 16, V)) * (V - 1), rng.integers(0, V, (N, 8, 16, V)))
    own = np.where(rng.random((N, 8, P)) < 0.7, rng.integers(0, 2, (N, 8, P)) * (V - 1), rng.integers(0, V, (N, 8, P)))
    hold = np.where(rng.random((N, 8, P)) < 0.75, rng.integers(0, 2, (N, 8, P)) * (V - 1), rng.integers(0, V, (N, 8, P)))
    wall = rng.integers(0, 2, (N, 8, P)); wt = 255 * rng.integers(0, 2, (N, 8, 16)); wt[N - 1, 7] = 255; wt[N - 1, 0, 0] = 0
    for g in range(8):
        x[:, g, :, 0] = (0, 15, 0, 15)[g % 4]; x[:, g, :, V - 1] = (15, 0, 0, 15)[g % 4]
    x[:, 7, :, 0] = 0; x[:, 7, :, 4] = 0; x[:, 7, :, V - 1] = 15
    kin[:, 7, :, V - 1] = V - 1; kin[:, 7, :, 0] = 0; kin[:, 7, 0::2, 2] = 4; kin[:, 7, 1::2, 2] = 0
    own[:, 7, 0] = V - 1; price[:, 7, :, 0] = 0; wall[:, 7, 0] = 0
    own[:, 7, P - 8:] = V - 1; hold[:, 7, P - 8:] = V - 1; wall[:, 7, P - 8:] = 1
    own[:, 7, P - 16:P - 8] = 0; own[:, 7, P - 24:P - 16] = 2; price[:, 7, :, P - 24:] = 15
    x[:, 5, :, V - 2] = 0; kin[:, 5, :, V - 2] = V - 2; own[:, 5, P - 2:] = V - 2; wall[:, 5, P - 2:] = 0; price[:, 5, :, P - 2:] = 15
    y = 15 >> (T // TL); s = [a for a in range(V, 61201, M) if a % y == 0][0] // y
    for r in range(N):
        wt[r, 5] = rng.permutation(np.array([255] * (s // 255) + [s % 255] + [0] * (15 - s // 255)))
    return pack(x, kin, own, hold, wall, price, wt)
def setup_inputs_spread(rng):
    def skew(top, p, *shape):
        return np.minimum(np.floor(top * rng.random(shape) ** p), top - 1).astype(np.int64)
    x = skew(16, np.exp2(rng.integers(-2, 4, (N, 8, 1, V)) + rng.integers(0, 2, (N, 8, 16, 1))), N, 8, 16, V)
    price = skew(16, np.exp2(rng.integers(-3, 3, (N, 8, 1, P)) + rng.integers(0, 2, (N, 8, 16, 1))), N, 8, 16, P)
    kin = skew(V, np.exp2(rng.integers(-1, 4, (N, 8, 16, 1))), N, 8, 16, V)
    own = skew(V, np.exp2(rng.integers(-2, 4, (N, 8, 1))), N, 8, P); hold = skew(V, np.exp2(rng.integers(-3, 4, (N, 8, 1))), N, 8, P)
    wall = (rng.random((N, 8, P)) < rng.choice(np.array([0.1, 0.5, 0.9]), (N, 8, 1))).astype(np.int64)
    wt = np.minimum(np.floor(np.exp2(8.02 * rng.random((N, 8, 16)))).astype(np.int64) - 1, 255)
    return pack(x, kin, own, hold, wall, price, wt)
def setup_inputs_ties(rng):
    x, kin, own, hold, wall, price, wt = parts(rng)
    n = Q - 2 + rng.integers(0, 2, (N, 8, 1, V)) + (rng.random((N, 8, 1, V)) < 0.03) + (np.arange(8) % 2).reshape(1, 8, 1, 1)
    x = 6 + (np.argsort(rng.random((N, 8, 16, V)), axis=2) < n).astype(np.int64)
    price = np.broadcast_to(rng.choice(np.array([6, 7, 7, 7, 7, 7, 7, 8]), (N, 8, 1, P)), (N, 8, 16, P)).copy()
    i = int(rng.integers(0, 16)); x[:, 6, :, V - 1] = 11; x[:, 6, i, V - 1] = 1
    k6 = kin[:, 6]; k6[k6 == V - 1] = V - 2; kin[:, 6, :, V - 1] = V - 1
    o6 = own[:, 6]; o6[o6 == V - 1] = 0; own[:, 6, P - 2:] = V - 1; wall[:, 6] = 0; price[:, 6, :, P - 2:] = 15
    ya, yz = 15, 15
    for _ in range(T // TL):
        ya, yz = (ya + 11) >> 1, (yz + 1) >> 1
    for r in range(N):
        s = 32768 if r % 2 == 0 else 7 * M
        c = [a for a in range(256) if (s - yz * a) % ya == 0][0]; rest = (s - yz * c) // ya
        wt[r, 6] = np.insert(rng.permutation(np.array([255] * (rest // 255) + [rest % 255] + [0] * (14 - rest // 255))), i, c)
    return pack(x, kin, own, hold, wall, price, wt)
def check_inputs(d):
    bad = []
    for k, hi in (("x", 15), ("kin", V - 1), ("own", V - 1), ("hold", V - 1), ("wall", 1), ("price", 15), ("wt", 255)):
        a = np.asarray(d[k]).astype(np.float64)
        if not (np.min(a) >= 0 and np.max(a) <= hi): bad.append("range of " + k)
        elif np.any(a != np.floor(a)): bad.append("whole numbers in " + k)
    return bad
def reference(x, kin, own, hold, wall, price, wt):
    X = x.astype(np.float32).astype(np.int32).reshape(N, 8, 16, V); K = kin.astype(np.int64).reshape(N, 8, 16, V)
    heir = np.tile(np.arange(V), (N, 8, 1)); lane = np.arange(P)
    e = np.stack([gentries(a) for a in own]).astype(np.int64); h = np.stack([gentries(a) for a in hold]).astype(np.int64); wl = np.stack([gentries(a) for a in wall])
    y = price.astype(np.float32).astype(np.int32).reshape(N, 8, 16, P); w = wt.astype(np.int64).reshape(N, 8, 16, 1)
    for t in range(T):
        for r in range(N):
            s = (r + t) % N; XS, KS, HS, ys, hs, es = X[s], K[s], heir[s], y[r], h[r], e[r].copy()
            c = np.take_along_axis(KS, es[:, None, :], 2)
            d = np.take_along_axis(XS, c.reshape(8, 1, 16 * P), 2).reshape(8, 16, 16, P) - ys[:, :, None, :]
            solvent = np.add.reduce((d >= 0).astype(np.int32), axis=1) >= Q; score = np.add.reduce(np.abs(d), axis=1)
            offers = np.any(solvent, axis=1)
            k = np.where(offers, np.argmax(solvent, axis=1), np.argmin(score, axis=1))
            b = np.take_along_axis(c, k[:, None, :], 1)[:, 0]
            key = np.where(offers, b, V + es)
            first = np.argmax(key[:, :, None] == key[:, None, :], axis=2) == lane
            fg, fp = np.nonzero(first & ~offers); ef, f = es[fg, fp], b[fg, fp]
            KS[fg, 1::2, ef] = KS[fg, 1::2, f]
            HS[fg, ef] = f
            wg, wp = np.nonzero(first & offers); cw = b[wg, wp]
            XS[wg, :, cw] = np.maximum(XS[wg, :, cw] - (ys[wg, :, wp] >> 2), 0)
            ys[wg, :, wp] = np.minimum(ys[wg, :, wp] + 1, 15); hs[wg, wp] = cw
            es = np.take_along_axis(HS, es, 1)
            if t % TL == TL - 1:
                es = np.where(wl[r] == 1, hs, es)
                y[r] = (ys + np.take_along_axis(XS, es[:, None, :], 2)) >> 1
                u = np.add.reduce(w[s] * y[r], axis=1) & (M - 1)
                h[r] = np.where(u >= V, u - V, u)
            e[r] = es
    yk = np.add.reduce(K * np.arange(1, 17).reshape(1, 1, 16, 1), axis=2)
    return {"yx": X.reshape(N, 128, V).astype(np.float32).astype(BF), "yk": yk.astype(np.float32), "yh": heir.astype(np.float32), "yo": e.astype(np.float32), "yt": h.astype(np.float32)}

@@ -1,0 +1,416 @@
+from concourse.mybir import dt, AluOpType as OP, AxisListType as AX, ActivationFunctionType as AF
+
+V, P, T9, W = 1792, 256, 9, 2048
+BIG = float(1 << 20)
+MAGIC = 1.5 * (1 << 23) * 64
+KV = 9
+GRAM = [("B3", "s", (15, 14)), ("B4", "v", (10, 9, 5)), ("B5", "s", (13, 12)), ("B6", "v", (8, 7, 6)), ("B7", "s", (11,)), ("B0", "v", (4, 3, 2, 1, 0))]
+NV = 11
+
+F32, BF16, F16, I32, U16 = "float32", "bfloat16", "float16", "int32", "uint16"
+SCRATCH = {"B%d" % i: ("psum", [128, 512], F32) for i in range(8)}
+for _n, _s, _d in [
+        ("X", [W], F32), ("K", [W], F32), ("HE", [W], F32), ("IDT", [W], F32), ("IND", [W], BF16), ("BT", [3584], BF16),
+        ("kinb", [V], I32), ("xb", [V], BF16), ("ownb", [16], I32), ("holdb", [16], I32), ("wallb", [16], I32), ("wtb", [1], I32), ("prb", [P], BF16),
+        ("Yl", [9, P], BF16), ("Yo", [9, P], BF16), ("El", [9, 16], U16), ("Eo", [9, 16], U16), ("Hl", [9, 16], U16), ("Ho", [9, 16], U16),
+        ("Wo", [16], U16), ("W1", [16], U16), ("W2", [16], U16),
+        ("yexp", [16 * P], BF16), ("cU", [P], U16), ("c16", [P], F16), ("Em", [16, 32], F16), ("cm", [P], F32),
+        ("DL", [16 * P], F16), ("AB", [16, P], F16), ("s64", [16, 16], F32), ("low", [16, 16], F32), ("mm", [16, 16], F32), ("key", [16, 16], F32),
+        ("t8", [16, 8], F32), ("t4", [16, 4], F32), ("t2", [16, 2], F32), ("keyi", [16], I32), ("bi", [16], I32), ("Ff", [16], F32), ("FE", [16], F32),
+        ("dk", [16], U16), ("bu", [16], U16), ("ef", [16], F32), ("e17", [16], F32), ("FD", [16], F32), ("A1", [16], F32), ("Of", [16], F32), ("OD", [16], F32),
+        ("A2", [16], F32), ("C", [P], BF16), ("BDC", [16, 128], BF16), ("D", [16], F32), ("junk", [16, P], BF16), ("Db", [16], F32), ("nd", [16], F32), ("o1", [16], U16), ("o2", [16], U16),
+        ("fr", [P], F32), ("KF", [P], F32), ("yqa", [P], F32), ("yq", [P], F32), ("diff", [P], F32), ("YR", [P], F32),
+        ("em", [P], F32), ("e8", [128], F32), ("e4", [64], F32), ("e2", [32], F32), ("e1", [16], F32), ("e1n", [16], F32),
+        ("hf", [16], F32), ("bh", [16], F32), ("R", [16], F32), ("Rb", [16], F32), ("hn", [16], F32), ("hw", [16], F32), ("wf", [16], F32), ("nw", [16], F32),
+        ("ti", [P], I32), ("ti2", [P], I32), ("si", [16], I32), ("si2", [16], I32), ("si3", [16], F32),
+        ("pidx", [1], I32), ("cols", [32], F32), ("ints", [8], I32), ("i8", [8], F32), ("GM", [8], F32), ("m1", [8], F32), ("m2", [8], F32),
+        ("k16", [P], F32), ("DELTA", [P], F32), ("OH", [16], F16), ("SEL", [16, 128], F16), ("SELW", [16, 128], BF16), ("IDN", [128], F16), ("KKC", [P], F16),
+        ("i128", [128], F32), ("POS", [P], F32), ("PJ", [16], F32), ("BIAS", [16], F32), ("DJ", [16], F32), ("ONES", [P], F32),
+        ("WI", [520], F32), ("WB", [520], I32), ("WC", [520], I32), ("LOWC", [512], BF16), ("HIGH", [8], F32), ("KW", [8], F16),
+        ("K16", [V], F16), ("yxo", [V], BF16), ("yko", [V], F32), ("ro", [2, P], F32)]:
+    SCRATCH[_n] = ("sbuf", [128] + _s, _d)
+SEMAPHORES = ["v", "s", "p", "g", "lsem", "w1", "w2", "outs"] + ["ld%d" % i for i in range(7)] + [a + str(t) for a in "yeh" for t in range(1, T9)]
+
+
+def rank_program(g, core, T, topo):
+    rank = T.rank_of(core)
+    if rank is None:
+        return
+    n = len(T.cores)
+    eng = {"v": g.vector, "s": g.scalar, "p": g.tensor, "g": g, "y": g.sync}
+    cnt = {}
+    known = {q: {} for q in eng}
+    snap = {}
+    wr, rd = {}, {}
+
+    def need(q, ev):
+        _, sem, val = ev
+        if known[q].get(sem, 0) < val:
+            eng[q].wait_ge(T.sem[sem], val)
+            for s2, v2 in list(snap.get((sem, val), {}).items()) + [(sem, val)]:
+                if known[q].get(s2, 0) < v2:
+                    known[q][s2] = v2
+
+    def before(q, r, w):
+        evs = []
+        for k in r:
+            if k in wr:
+                evs.append(wr[k])
+        for k in w:
+            if k in wr:
+                evs.append(wr[k])
+            for e in rd.get(k, []):
+                if e[0] != q:
+                    evs.append(e)
+        best = {}
+        for e in evs:
+            if e[1] not in best or best[e[1]][2] < e[2]:
+                best[e[1]] = e
+        for e in sorted(best.values(), key=lambda e: -e[2]):
+            need(q, e)
+
+    def after(ev, r, w):
+        for k in r:
+            rd.setdefault(k, []).append(ev)
+        for k in w:
+            wr[k] = ev
+            rd[k] = []
+
+    def op(q, r, w, fn):
+        before(q, r, w)
+        i = fn(eng[q])
+        cnt[q] = cnt.get(q, 0) + 1
+        i.then_inc(T.sem[q], 1)
+        ev = (q, q, cnt[q])
+        snap[(q, cnt[q])] = dict(known[q])
+        after(ev, r, w)
+
+    def dma(q, r, w, sem, out, in_):
+        before(q, r, w)
+        eng[q].dma_start(out, in_).then_inc(T.sem[sem], 16)
+        cnt[sem] = cnt.get(sem, 0) + 16
+        snap[(sem, cnt[sem])] = dict(known[q])
+        after(("dma", sem, cnt[sem]), r, w)
+
+    def send(dst, r, out, in_, sem):
+        before("g", r, [])
+        rid, pid = topo.addr(dst, core)
+        m = topo.mask(core, dst)
+        g.remote_dma(out, in_, T.sem[sem], T.sem.lsem, pid, rid, m)
+        cnt["lsem"] = cnt.get("lsem", 0) + len(topo.engines(core, dst))
+
+    def landing(src, w, sem):
+        val = len(topo.engines(src, core))
+        for k in w:
+            wr[k] = ("remote", sem, val)
+            rd[k] = []
+
+    def ts(q, r, w, out, in0, s1, s2, o0, o1=None):
+        if o1 is None:
+            op(q, r, w, lambda e: e.tensor_scalar(out, in0, s1, None, o0))
+        else:
+            op(q, r, w, lambda e: e.tensor_scalar(out, in0, s1, s2, o0, o1))
+
+    def tt(r, w, out, in0, in1, o):
+        op("v", r, w, lambda e: e.tensor_tensor(out, in0, in1, o))
+
+    def cp(r, w, out, in_):
+        op("v", r, w, lambda e: e.tensor_copy(out, in_))
+
+    def act(r, w, out, in_, f, **kw):
+        op("s", r, w, lambda e: e.activation(out, in_, f, **kw))
+
+    def fill(w, ap, c):
+        op("v", [], w, lambda e: e.memset(ap, c))
+
+    nxt, prv = T.cores[(rank + 1) % n], T.cores[(rank - 1) % n]
+    nx2, pv2 = T.cores[(rank + 2) % n], T.cores[(rank - 2) % n]
+
+    dma("y", [], ["ownb"], "ld0", T.ownb[:], T.own[:])
+    dma("y", [], ["kinb"], "ld1", T.kinb[:], T.kin[:])
+    dma("s", [], ["prb"], "ld2", T.prb[:], T.price[:])
+    dma("s", [], ["xb"], "ld3", T.xb[:], T.x[:])
+    dma("y", [], ["wallb"], "ld4", T.wallb[:], T.wall[:])
+    dma("y", [], ["holdb"], "ld5", T.holdb[:], T.hold[:])
+    dma("y", [], ["wtb"], "ld6", T.wtb[:], T.wt[:])
+
+    def iota(k, out, pat, base, cm, f=True):
+        op("g", [], [k], lambda e: e.iota(out, pat, base, cm, allow_small_or_imprecise_dtypes=f))
+    iota("pidx", T.pidx[:], [[0, 1]], 0, 1, False)
+    iota("i8", T.i8[:], [[1, 8]], 0, 0)
+    iota("k16", T.k16[:], [[0, 16], [1, 16]], 0, 0)
+    iota("WI", T.WI[:, 0:512], [[1, 512]], 0, 0)
+    iota("WI2", T.WI[:, 512:520], [[512, 8]], 0, 0)
+    iota("PJ", T.PJ[:], [[16, 16]], 0, 0)
+    iota("i128", T.i128[:], [[1, 128]], 0, 0)
+    iota("POS", T.POS[:], [[1, P]], 0, 0)
+    iota("IDT", T.IDT[:], [[1, W]], 0, 0)
+
+    col = {}
+
+    def c_(name):
+        col.setdefault(name, len(col))
+        i = col[name]
+        return T.cols[:, i:i + 1]
+    ii, gi = T.ints[:, 0:1], T.ints[:, 1:2]
+    ts("v", ["pidx"], ["ii"], ii, T.pidx[:], 15, None, OP.bitwise_and)
+    ts("v", ["pidx"], ["gi"], gi, T.pidx[:], 4, None, OP.logical_shift_right)
+    cp(["pidx"], ["pF"], c_("pF"), T.pidx[:])
+    cp(["ii"], ["iF"], c_("iF"), ii)
+    cp(["gi"], ["gF"], c_("gF"), gi)
+    for b in range(4):
+        ts("v", ["ii"], ["ib%d" % b], T.ints[:, 2 + b:3 + b], ii, b, 1, OP.logical_shift_right, OP.bitwise_and)
+    ts("v", ["gi"], ["gb"], T.ints[:, 6:7], gi, 1, None, OP.bitwise_and)
+    for b in range(4):
+        ts("v", ["ib%d" % b], ["pb%d" % b], c_("pb%d" % b), T.ints[:, 2 + b:3 + b], 2.0 ** -(1 << b) - 1.0, 1.0, OP.mult, OP.add)
+    cp(["ib0"], ["odd"], c_("odd"), T.ints[:, 2:3])
+    ts("v", ["ib0"], ["even"], c_("even"), T.ints[:, 2:3], -1.0, 1.0, OP.mult, OP.add)
+    cp(["gb"], ["gO"], c_("gO"), T.ints[:, 6:7])
+    ts("v", ["gb"], ["gE"], c_("gE"), T.ints[:, 6:7], -1.0, 1.0, OP.mult, OP.add)
+    tt(["pb0", "pb1"], ["pa"], c_("pa"), c_("pb0"), c_("pb1"), OP.mult)
+    tt(["pb2", "pb3"], ["pc"], c_("pc"), c_("pb2"), c_("pb3"), OP.mult)
+    ts("v", ["iF"], ["l9"], c_("l9"), c_("iF"), 9.0, None, OP.is_lt)
+    ts("v", ["iF"], ["l12"], c_("l12"), c_("iF"), 12.0, None, OP.is_lt)
+    ts("v", ["iF"], ["b12"], c_("b12"), c_("iF"), 12.0, BIG, OP.is_equal, OP.mult)
+    ts("v", ["iF"], ["q12"], c_("q12"), c_("iF"), 12.0, -1.0 / 256, OP.is_equal, OP.mult)
+    tt(["pa", "pc"], ["pw"], c_("pw"), c_("pa"), c_("pc"), OP.mult)
+    ts("v", ["l12"], ["s12"], c_("s12"), c_("l12"), BIG, None, OP.mult)
+    ts("v", ["l9"], ["l9d"], c_("l9d"), c_("l9"), 2.0, None, OP.mult)
+    ts("v", ["l9"], ["l9n"], c_("l9n"), c_("l9"), -1.0, None, OP.mult)
+    tt(["l12", "l9"], ["h3"], c_("h3"), c_("l12"), c_("l9"), OP.subtract)
+    ts("v", ["iF"], ["i1"], c_("i1"), c_("iF"), 1.0, None, OP.add)
+    ts("v", ["pw"], ["ph"], c_("ph"), c_("pw"), 0.5, -0.5, OP.mult, OP.add)
+    ts("v", ["h3"], ["h3d"], c_("h3d"), c_("h3"), 2.0, None, OP.mult)
+    ts("v", ["h3"], ["h3n"], c_("h3n"), c_("h3"), -1.0, None, OP.mult)
+    ts("v", ["i8", "gF"], ["GM"], T.GM[:], T.i8[:], c_("gF"), None, OP.is_equal)
+    ts("v", ["k16", "iF"], ["OH"], T.OH[:], T.k16[:, 0:16], c_("iF"), None, OP.is_equal)
+    ts("v", ["k16", "iF"], ["DELTA"], T.DELTA[:], T.k16[:], c_("iF"), None, OP.is_equal)
+    ts("v", ["k16"], ["KKC"], T.KKC[:], T.k16[:], 1024.0, None, OP.mult)
+    ts("v", ["i128", "pF"], ["IDN"], T.IDN[:], T.i128[:], c_("pF"), None, OP.is_equal)
+    sel = ["SEL%d" % r for r in range(16)]
+    fill(sel, T.SEL[:], 0.0)
+    for r in range(16):
+        cp(["GM"], ["SEL%d" % r], T.SEL[:, r, r:128:16], T.GM[:])
+
+    cp(["ownb"], ["El0"], T.El[:, 0, :], T.ownb[:])
+    ts("v", ["prb"], ["Yl0"], T.Yl[:, 0, :], T.prb[:], 64.0, None, OP.mult)
+    cp(["kinb"], ["K"], T.K[:, 0:V], T.kinb[:])
+    fill(["K"], T.K[:, V:W], 0.0)
+    fill(["X"], T.X[:, V:W], 1.0)
+    act(["xb"], ["X"], T.X[:, 0:V], T.xb[:], AF.Copy, scale=64.0, bias=1.0)
+    cp(["wallb"], ["Wo"], T.Wo[:], T.wallb[:])
+    send(nxt, ["Wo"], T.W1[:], T.Wo[:], "w1")
+    send(nx2, ["Wo"], T.W2[:], T.Wo[:], "w2")
+    landing(prv, ["W1"], "w1")
+    landing(pv2, ["W2"], "w2")
+    cp(["holdb"], ["Hl0"], T.Hl[:, 0, :], T.holdb[:])
+
+    def late_constants():
+        ts("v", ["WI", "pw", "ph"], ["WB"], T.WB[:, 0:512], T.WI[:, 0:512], c_("pw"), c_("ph"), OP.mult, OP.add)
+        ts("v", ["WI2", "pw", "ph"], ["WB2"], T.WB[:, 512:520], T.WI[:, 512:520], c_("pw"), c_("ph"), OP.mult, OP.add)
+        ts("v", ["WB", "WB2"], ["WC"], T.WC[:], T.WB[:], 1, None, OP.bitwise_and)
+        ts("v", ["WC", "l9d", "l9n"], ["LOWC"], T.LOWC[:], T.WC[:, 0:512], c_("l9d"), c_("l9n"), OP.mult, OP.add)
+        ts("v", ["WC", "h3d", "h3n"], ["HIGH"], T.HIGH[:], T.WC[:, 512:520], c_("h3d"), c_("h3n"), OP.mult, OP.add)
+        for u in range(7):
+            ts("v", ["LOWC", "HIGH"], ["BT%d" % u], T.BT[:, 512 * u:512 * u + 512], T.LOWC[:], T.HIGH[:, u:u + 1], None, OP.add)
+        ts("v", ["POS", "q12"], ["POS"], T.POS[:], T.POS[:], c_("q12"), None, OP.mult)
+        ts("v", ["GM", "s12"], ["m1"], T.m1[:], T.GM[:], c_("s12"), None, OP.mult)
+        ts("v", ["GM", "b12"], ["m2"], T.m2[:], T.GM[:], c_("b12"), None, OP.mult)
+        ts("v", ["GM", "i1"], ["KW"], T.KW[:], T.GM[:], c_("i1"), None, OP.mult)
+        ts("v", ["PJ", "iF"], ["PJ"], T.PJ[:], T.PJ[:], c_("iF"), None, OP.add)
+        ts("v", ["PJ"], ["BIAS"], T.BIAS[:], T.PJ[:], BIG / 256, -12.0 * BIG, OP.mult, OP.add)
+        ts("v", ["PJ"], ["DJ"], T.DJ[:], T.PJ[:], float(V), None, OP.add)
+        fill(["ONES"], T.ONES[:], 1.0)
+        fill(["IND"], T.IND[:, 0:V], 64.0)
+        fill(["IND"], T.IND[:, V:W], 0.0)
+        act(["IDT"], ["HE"], T.HE[:], T.IDT[:], AF.Copy)
+
+    for t in range(T9):
+        jub, last = t % 3 == 2, t == T9 - 1
+        Yt, Et, Ht = "Yl%d" % t, "El%d" % t, "Hl%d" % t
+        if t:
+            landing(prv, [Yt], "y%d" % t)
+            landing(prv, [Et], "e%d" % t)
+            landing(prv, [Ht], "h%d" % t)
+        yv, eu, hv = T.Yl[:, t, :], T.El[:, t, :], T.Hl[:, t, :]
+        for k in range(16):
+            if k < KV:
+                cp([Yt], ["yx%d" % k], T.yexp[:, k:16 * P:16], yv)
+            else:
+                act([Yt], ["yx%d" % k], T.yexp[:, k:16 * P:16], yv, AF.Copy)
+        cp(["K", Et], ["cU"], T.cU[:], T.K[:].indirect(eu))
+        act(["K", Et], ["c16"], T.c16[:], T.K[:].indirect(eu), AF.Copy)
+        act(["c16", "gE"], ["Em0"], T.Em[:, :, 0:16], T.c16[:], AF.Copy, scale=c_("gE"))
+        act(["c16", "gO"], ["Em1"], T.Em[:, :, 16:32], T.c16[:], AF.Copy, scale=c_("gO"))
+
+        def kc(e):
+            e.matmul(T.B2[:, 0:P], T.IDN[:], T.KKC[:], True, False)
+            for A in range(4):
+                s = slice(32 * A, 32 * A + 32)
+                for a in range(16):
+                    e.matmul(T.B2[s, 16 * a:16 * a + 16], T.Em[s, a, :], T.OH[s, :], False, False)
+            return e.matmul(T.B2[:, 0:P], T.IDN[:], T.KKC[:], False, True)
+        op("p", ["Em0", "Em1", "OH", "IDN", "KKC"], ["B2"], kc)
+        for ch in range(4):
+            s, f = slice(4 * ch, 4 * ch + 4), slice(1024 * ch, 1024 * ch + 1024)
+            tt(["X", "cU"] + ["yx%d" % k for k in range(16)], ["DL%d" % ch], T.DL[:, f], T.X[:].indirect(T.cU[:, 64 * ch:64 * ch + 64]), T.yexp[:, f], OP.subtract)
+            act(["DL%d" % ch], ["AB%d" % ch], T.AB[:, s, :], T.DL[:, f], AF.Abs)
+            zb, o = ("B0", "B1")[ch // 2], 64 * (ch % 2)
+
+            def zsum(e):
+                for r in range(16):
+                    i = e.matmul(T[zb][:, o:o + 64], T.SEL[:, r, :], T.AB[:, s, 16 * r:16 * r + 16], r == 0, r == 15)
+                return i
+            op("p", ["AB%d" % ch] + sel, [zb], zsum)
+        if t == 0:
+            late_constants()
+        act([Yt], ["yqa"], T.yqa[:], yv, AF.Copy, scale=0.25, bias=-24.0)
+        act(["c16", "even"], ["cm"], T.cm[:], T.c16[:], AF.Copy, scale=c_("even"))
+        cp([Et], ["ef"], T.ef[:], eu)
+        ts("v", [Et], ["e17"], T.e17[:], eu, float(V), None, OP.add)
+        for h in range(2):
+            zb, s, x = ("B0", "B1")[h], slice(8 * h, 8 * h + 8), str(h)
+            z = T[zb][:, 0:128]
+            ts("v", [zb], ["s64" + x], T.s64[:, s, :], z, MAGIC, -MAGIC, OP.add, OP.add)
+            tt([zb, "s64" + x], ["low" + x], T.low[:, s, :], z, T.s64[:, s, :], OP.subtract)
+            ts("v", ["low" + x], ["mm" + x], T.mm[:, s, :], T.low[:, s, :], 4.0, 512.0, OP.is_lt, OP.mult)
+            tt(["mm" + x, "s64" + x], ["mm" + x], T.mm[:, s, :], T.mm[:, s, :], T.s64[:, s, :], OP.mult)
+            tt(["mm" + x, "B2"], ["key" + x], T.key[:, s, :], T.mm[:, s, :], T.B2[:, 128 * h:128 * h + 128], OP.add)
+            tt(["key" + x], ["t8" + x], T.t8[:, s, :], T.key[:, s, 0:8], T.key[:, s, 8:16], OP.min)
+            tt(["t8" + x], ["t4" + x], T.t4[:, s, :], T.t8[:, s, 0:4], T.t8[:, s, 4:8], OP.min)
+            tt(["t4" + x], ["t2" + x], T.t2[:, s, :], T.t4[:, s, 0:2], T.t4[:, s, 2:4], OP.min)
+            tt(["t2" + x], ["keyi" + x], T.keyi[:, s], T.t2[:, s, 0], T.t2[:, s, 1], OP.min)
+        ky = ["keyi0", "keyi1"]
+        ts("v", ky, ["Ff"], T.Ff[:], T.keyi[:], 32768.0, None, OP.is_ge)
+        ts("v", ky, ["bi"], T.bi[:], T.keyi[:], 2047, None, OP.bitwise_and)
+        tt(["Ff", "e17"], ["FE"], T.FE[:], T.Ff[:], T.e17[:], OP.mult)
+        cp(["bi"], ["bu"], T.bu[:], T.bi[:])
+        tt(["bi", "FE"], ["dk"], T.dk[:], T.bi[:], T.FE[:], OP.max)
+        tt(["BT%d" % u for u in range(7)] + ["dk", "POS"], ["C"], T.C[:], T.BT[:].indirect(T.dk[:]), T.POS[:], OP.add)
+        act(["IDT", "bu"], ["fr"], T.fr[:], T.IDT[:].indirect(T.bu[:]), AF.Copy)
+        for q in range(8):
+            if q < 5:
+                ts("v", ["C", "m1", "m2"], ["BD%d" % q], T.BDC[:, :, 16 * q:16 * q + 16], T.C[:], T.m1[:, q:q + 1], T.m2[:, q:q + 1], OP.mult, OP.add)
+            else:
+                act(["C", "m1", "m2"], ["BD%d" % q], T.BDC[:, :, 16 * q:16 * q + 16], T.C[:], AF.Identity, scale=T.m1[:, q:q + 1], bias=T.m2[:, q:q + 1])
+        for bank, q, aa in GRAM:
+            def gram(e):
+                o = 0
+                for a in aa:
+                    i = e.matmul(T[bank][:, o:o + 16 * a + 16], T.BDC[:, a, :], T.C[:, 0:16 * a + 16], True, True)
+                    o += 16 * a + 16
+                return i
+            op("p", ["C"] + ["BD%d" % i for i in range(8)], [bank], gram)
+        ts("v", ky, ["Of"], T.Of[:], T.keyi[:], 32768.0, None, OP.is_lt)
+        tt(["Ff", "DJ"], ["FD"], T.FD[:], T.Ff[:], T.DJ[:], OP.mult)
+        tt(["Of", "DJ"], ["OD"], T.OD[:], T.Of[:], T.DJ[:], OP.mult)
+        tt(["FD", "bi"], ["A1"], T.A1[:], T.bi[:], T.FD[:], OP.max)
+        tt(["OD", "ef"], ["A2"], T.A2[:], T.ef[:], T.OD[:], OP.max)
+        ts("v", ["yqa"], ["yq"], T.yq[:], T.yqa[:], MAGIC, -MAGIC, OP.add, OP.add)
+        tt(["X", "bu", "yq"], ["diff"], T.diff[:], T.X[:].indirect(T.bu[:]), T.yq[:], OP.subtract)
+        for bank, q, aa in GRAM:
+            o = 0
+            for a in aa:
+                z = T[bank][:, o:o + 16 * a + 16]
+                o += 16 * a + 16
+                if q == "v":
+                    op("v", [bank], ["D%d" % a], lambda e: e.tensor_reduce(T.D[:, a:a + 1], z, AX.X, OP.max))
+                else:
+                    act([bank, "BIAS"], ["D%d" % a, "junk%d" % a], T.junk[:, a, 0:16 * a + 16], z, AF.Relu, bias=T.BIAS[:, a:a + 1], accum_out=T.D[:, a:a + 1])
+        act(["K", "bu", "odd"], ["KF"], T.KF[:], T.K[:].indirect(T.bu[:]), AF.Copy, scale=c_("odd"))
+        dv, ds = ["D%d" % a for a in range(NV)], ["D%d" % a for a in range(NV, 16)]
+        tt(dv + ["BIAS"], dv, T.D[:, 0:NV], T.D[:, 0:NV], T.BIAS[:, 0:NV], OP.add)
+        tt(dv + ds + ["DJ"], ["nd"], T.nd[:], T.D[:], T.DJ[:], OP.min)
+        tt(["nd", "A2"], ["o2"], T.o2[:], T.A2[:], T.nd[:], OP.max)
+        tt(["nd", "A1"], ["o1"], T.o1[:], T.A1[:], T.nd[:], OP.max)
+
+        def redeem_prices(k, out):
+            tt(["IND", "o1", Yt], ["YR"], T.YR[:], T.IND[:].indirect(T.o1[:]), yv, OP.add)
+            ts("v", ["YR"], [k], out, T.YR[:], 960.0, None, OP.min)
+
+        def redeem_wealth():
+            tt(["diff", "o1", "ONES"], ["X"], T.X[:].indirect(T.o1[:]), T.diff[:], T.ONES[:], OP.max)
+
+        def kin_lines():
+            tt(["KF", "cm", "o2"], ["K"], T.K[:].indirect(T.o2[:]), T.KF[:], T.cm[:], OP.add)
+
+        def holders():
+            cp([Ht], ["hf"], T.hf[:], hv)
+            ts("v", ["o1"], ["R"], T.R[:], T.o1[:], float(V), None, OP.is_lt)
+            tt(["bi", "hf"], ["bh"], T.bh[:], T.bi[:], T.hf[:], OP.subtract)
+            tt(["R", "bh"], ["Rb"], T.Rb[:], T.R[:], T.bh[:], OP.mult)
+
+        cp(["fr", "o2"], ["HE"], T.HE[:].indirect(T.o2[:]), T.fr[:])
+        Yk, Ek, Hk = "Yo%d" % t, "Eo%d" % t, "Ho%d" % t
+        yo, eo, ho = T.Yo[:, t, :], T.Eo[:, t, :], T.Ho[:, t, :]
+        if not jub:
+            redeem_prices(Yk, yo)
+            send(nxt, [Yk], T.Yl[:, t + 1, :], yo, "y%d" % (t + 1))
+        else:
+            redeem_prices("y1", T.prb[:])
+            redeem_wealth()
+            wl, wk = ((T.W2, "W2"), (T.W1, "W1"), (T.Wo, "Wo"))[t // 3]
+            cp([wk], ["wf"], T.wf[:], wl[:])
+            ts("v", [wk], ["nw"], T.nw[:], wl[:], -1.0, 1.0, OP.mult, OP.add)
+            holders()
+            tt(["Rb", "hf"], ["hn"], T.hn[:], T.Rb[:], T.hf[:], OP.add)
+            tt(["hn", "wf"], ["hw"], T.hw[:], T.hn[:], T.wf[:], OP.mult)
+        tt(["HE", Et, "DELTA"], ["em"], T.em[:], T.HE[:].indirect(eu), T.DELTA[:], OP.mult)
+        tt(["em"], ["e8"], T.e8[:], T.em[:, 0:256:2], T.em[:, 1:256:2], OP.add)
+        tt(["e8"], ["e4"], T.e4[:], T.e8[:, 0:128:2], T.e8[:, 1:128:2], OP.add)
+        tt(["e4"], ["e2"], T.e2[:], T.e4[:, 0:64:2], T.e4[:, 1:64:2], OP.add)
+        if not jub:
+            tt(["e2"], [Ek], eo, T.e2[:, 0:32:2], T.e2[:, 1:32:2], OP.add)
+            send(nxt, [Ek], T.El[:, t + 1, :], eo, "e%d" % (t + 1))
+            redeem_wealth()
+            kin_lines()
+            holders()
+            tt(["Rb", "hf"], [Hk], ho, T.Rb[:], T.hf[:], OP.add)
+            send(nxt, [Hk], T.Hl[:, t + 1, :], ho, "h%d" % (t + 1))
+        else:
+            tt(["e2"], ["e1"], T.e1[:], T.e2[:, 0:32:2], T.e2[:, 1:32:2], OP.add)
+            tt(["e1", "nw"], ["e1n"], T.e1n[:], T.e1[:], T.nw[:], OP.mult)
+            tt(["e1n", "hw"], [Ek], eo, T.e1n[:], T.hw[:], OP.max)
+            if not last:
+                send(nxt, [Ek], T.El[:, t + 1, :], eo, "e%d" % (t + 1))
+            tt(["X", Ek, "y1"], ["ti"], T.ti[:], T.X[:].indirect(eo), T.prb[:], OP.add)
+            ts("v", ["ti"], ["ti2"], T.ti2[:], T.ti[:], 7, None, OP.arith_shift_right)
+            ts("v", ["ti2"], [Yk], yo, T.ti2[:], 64.0, None, OP.mult)
+            if not last:
+                send(nxt, [Yk], T.Yl[:, t + 1, :], yo, "y%d" % (t + 1))
+            if t == 2:
+                cp(["wtb"], ["wtF"], c_("wtF"), T.wtb[:])
+                ts("v", sel + ["wtF"], ["SELW"], T.SELW[:], T.SEL[:], c_("wtF"), None, OP.mult)
+
+            def wsum(e):
+                for r in range(16):
+                    i = e.matmul(T.B2[:, 0:16], T.SELW[:, r, :], T.Yo[:, t, r:P:16], r == 0, r == 15)
+                return i
+            op("p", ["SELW", Yk], ["B2"], wsum)
+            kin_lines()
+            cp(["B2"], ["si"], T.si[:], T.B2[:, 0:16])
+            ts("v", ["si"], ["si2"], T.si2[:], T.si[:], 6, 2047, OP.logical_shift_right, OP.bitwise_and)
+            ts("v", ["si2"], ["si3"], T.si3[:], T.si2[:], float(V), -float(V), OP.is_ge, OP.mult)
+            tt(["si2", "si3"], [Hk], ho, T.si2[:], T.si3[:], OP.add)
+            if not last:
+                send(nxt, [Hk], T.Hl[:, t + 1, :], ho, "h%d" % (t + 1))
+
+    dma("y", ["HE"], [], "outs", T.yh[:], T.HE[0:128:16, 0:V])
+    act(["X"], ["yxo"], T.yxo[:], T.X[:, 0:V], AF.Copy, scale=1.0 / 64, bias=-1.0 / 64)
+    dma("y", ["yxo"], [], "outs", T.yx[:], T.yxo[:])
+    cp(["K"], ["K16"], T.K16[:], T.K[:, 0:V])
+    for q in range(4):
+        s = slice(448 * q, 448 * q + 448)
+        bk = "B%d" % (4 + q)
+        op("p", ["K16", "KW"], [bk], lambda e: e.matmul(T[bk][0:8, 0:448], T.KW[:], T.K16[:, s], True, True))
+    act(["IDT", "Eo8"], ["ro0"], T.ro[:, 0, :], T.IDT[:].indirect(T.Eo[:, 8, :]), AF.Copy)
+    act(["IDT", "Ho8"], ["ro1"], T.ro[:, 1, :], T.IDT[:].indirect(T.Ho[:, 8, :]), AF.Copy)
+    for q in range(4):
+        s = slice(448 * q, 448 * q + 448)
+        bk = "B%d" % (4 + q)
+        cp([bk], ["yko"], T.yko[0:8, s], T[bk][0:8, 0:448])
+    dma("y", ["ro0"], [], "outs", T.yo[:], T.ro[0:128:16, 0, :])
+    dma("y", ["ro1"], [], "outs", T.yt[:], T.ro[0:128:16, 1, :])
+    dma("y", ["yko"], [], "outs", T.yk[:], T.yko[0:8, :])
+    for sem in ("v", "s", "p", "g", "lsem", "outs"):
+        g.wait_ge(T.sem[sem], cnt[sem])

@@ -3,9 +3,10 @@ from concourse.mybir import dt, AluOpType as OP, AxisListType as AX, ActivationF
 V, P, T9, W = 1792, 256, 9, 2048
 BIG = float(1 << 20)
 MAGIC = 1.5 * (1 << 23) * 64
-KV = 9
-GRAM = [("B3", "s", (15, 14)), ("B4", "v", (10, 9, 5)), ("B5", "s", (13, 12)), ("B6", "v", (8, 7, 6)), ("B7", "s", (11,)), ("B0", "v", (4, 3, 2, 1, 0))]
-NV = 11
+KV = 11
+CHUNKS = [(0, 4), (4, 4), (8, 4), (12, 4)]
+GRAM = [[("B3", "v", (7, 6, 5)), ("B6", "v", (4, 3, 2, 1, 0))], [("B7", "s", (15, 14)), ("B5", "v", (11, 10, 8)), ("B0", "s", (13, 12)), ("B4", "v", (9,))]]
+NV = 12
 
 F32, BF16, F16, I32, U16 = "float32", "bfloat16", "float16", "int32", "uint16"
 SCRATCH = {"B%d" % i: ("psum", [128, 512], F32) for i in range(8)}
@@ -15,13 +16,13 @@ for _n, _s, _d in [
         ("Yl", [9, P], BF16), ("Yo", [9, P], BF16), ("El", [9, 16], U16), ("Eo", [9, 16], U16), ("Hl", [9, 16], U16), ("Ho", [9, 16], U16),
         ("Wo", [16], U16), ("W1", [16], U16), ("W2", [16], U16),
         ("yexp", [16 * P], BF16), ("cU", [P], U16), ("c16", [P], F16), ("Em", [16, 32], F16), ("cm", [P], F32),
-        ("DL", [16 * P], F16), ("AB", [16, P], F16), ("s64", [16, 16], F32), ("low", [16, 16], F32), ("mm", [16, 16], F32), ("key", [16, 16], F32),
-        ("t8", [16, 8], F32), ("t4", [16, 4], F32), ("t2", [16, 2], F32), ("keyi", [16], I32), ("bi", [16], I32), ("Ff", [16], F32), ("FE", [16], F32),
-        ("dk", [16], U16), ("bu", [16], U16), ("ef", [16], F32), ("e17", [16], F32), ("FD", [16], F32), ("A1", [16], F32), ("Of", [16], F32), ("OD", [16], F32),
-        ("A2", [16], F32), ("C", [P], BF16), ("BDC", [16, 128], BF16), ("D", [16], F32), ("junk", [16, P], BF16), ("Db", [16], F32), ("nd", [16], F32), ("o1", [16], U16), ("o2", [16], U16),
-        ("fr", [P], F32), ("KF", [P], F32), ("yqa", [P], F32), ("yq", [P], F32), ("diff", [P], F32), ("YR", [P], F32),
-        ("em", [P], F32), ("e8", [128], F32), ("e4", [64], F32), ("e2", [32], F32), ("e1", [16], F32), ("e1n", [16], F32),
-        ("hf", [16], F32), ("bh", [16], F32), ("R", [16], F32), ("Rb", [16], F32), ("hn", [16], F32), ("hw", [16], F32), ("wf", [16], F32), ("nw", [16], F32),
+        ("DL", [16 * P], F16), ("AB", [16, P], F16), ("s64", [P], F32), ("low", [P], F32), ("mm", [P], F32), ("key", [P], F32),
+        ("ks", [P], F32), ("RST", [128], F32), ("keyi", [32], I32), ("BE", [32], I32), ("FE", [16], F32), ("DJ2", [32], F32), ("A0", [32], F32), ("A12", [32], F32),
+        ("dk", [16], U16), ("bu", [16], U16), ("e17", [16], F32), ("VB", [1], F32), ("uB", [16], F32), ("hx", [16], F32),
+        ("C", [P], BF16), ("BDC", [16, 128], BF16), ("D", [16], F32), ("junk", [16, P], BF16), ("nd", [16], F32), ("o1", [16], U16), ("o2", [16], U16),
+        ("fr", [P], F32), ("KF", [P], F32), ("yqa", [P], F32), ("yqr", [P], F32), ("yq", [P], BF16), ("xg", [P], BF16), ("diff", [P], F32), ("red", [P], BF16), ("IDB", [128], BF16), ("NIB", [128], BF16),
+        ("em", [P], F32), ("es", [P], F32), ("NZ", [P], F32), ("e1n", [16], F32),
+        ("hn", [16], F32), ("hw", [16], F32), ("wf", [16], F32), ("nw", [16], F32),
         ("ti", [P], I32), ("ti2", [P], I32), ("si", [16], I32), ("si2", [16], I32), ("si3", [16], F32),
         ("pidx", [1], I32), ("cols", [32], F32), ("ints", [8], I32), ("i8", [8], F32), ("GM", [8], F32), ("m1", [8], F32), ("m2", [8], F32),
         ("k16", [P], F32), ("DELTA", [P], F32), ("OH", [16], F16), ("SEL", [16, 128], F16), ("SELW", [16, 128], BF16), ("IDN", [128], F16), ("KKC", [P], F16),
@@ -185,7 +186,7 @@ def rank_program(g, core, T, topo):
     ts("v", ["i8", "gF"], ["GM"], T.GM[:], T.i8[:], c_("gF"), None, OP.is_equal)
     ts("v", ["k16", "iF"], ["OH"], T.OH[:], T.k16[:, 0:16], c_("iF"), None, OP.is_equal)
     ts("v", ["k16", "iF"], ["DELTA"], T.DELTA[:], T.k16[:], c_("iF"), None, OP.is_equal)
-    ts("v", ["k16"], ["KKC"], T.KKC[:], T.k16[:], 1024.0, None, OP.mult)
+    ts("v", ["k16"], ["KKC"], T.KKC[:], T.k16[:], 1024.0, -16384.0, OP.mult, OP.add)
     ts("v", ["i128", "pF"], ["IDN"], T.IDN[:], T.i128[:], c_("pF"), None, OP.is_equal)
     sel = ["SEL%d" % r for r in range(16)]
     fill(sel, T.SEL[:], 0.0)
@@ -194,10 +195,11 @@ def rank_program(g, core, T, topo):
 
     cp(["ownb"], ["El0"], T.El[:, 0, :], T.ownb[:])
     ts("v", ["prb"], ["Yl0"], T.Yl[:, 0, :], T.prb[:], 64.0, None, OP.mult)
-    cp(["kinb"], ["K"], T.K[:, 0:V], T.kinb[:])
-    fill(["K"], T.K[:, V:W], 0.0)
-    fill(["X"], T.X[:, V:W], 1.0)
-    act(["xb"], ["X"], T.X[:, 0:V], T.xb[:], AF.Copy, scale=64.0, bias=1.0)
+    fill(["Kt"], T.K[:, V:W], 0.0)
+    fill(["Xt"], T.X[:, V:W], 1.0)
+    ts("v", ["xb"], ["Xa"], T.X[:, 0:768], T.xb[:, 0:768], 64.0, 1.0, OP.mult, OP.add)
+    act(["xb"], ["Xb"], T.X[:, 768:V], T.xb[:, 768:V], AF.Copy, scale=64.0, bias=1.0)
+    XK, KK = ["Xa", "Xb", "Xt"], ["K", "Kt"]
     cp(["wallb"], ["Wo"], T.Wo[:], T.wallb[:])
     send(nxt, ["Wo"], T.W1[:], T.Wo[:], "w1")
     send(nx2, ["Wo"], T.W2[:], T.Wo[:], "w2")
@@ -206,6 +208,7 @@ def rank_program(g, core, T, topo):
     cp(["holdb"], ["Hl0"], T.Hl[:, 0, :], T.holdb[:])
 
     def late_constants():
+        cp(["kinb"], ["K"], T.K[:, 0:V], T.kinb[:])
         ts("v", ["WI", "pw", "ph"], ["WB"], T.WB[:, 0:512], T.WI[:, 0:512], c_("pw"), c_("ph"), OP.mult, OP.add)
         ts("v", ["WI2", "pw", "ph"], ["WB2"], T.WB[:, 512:520], T.WI[:, 512:520], c_("pw"), c_("ph"), OP.mult, OP.add)
         ts("v", ["WB", "WB2"], ["WC"], T.WC[:], T.WB[:], 1, None, OP.bitwise_and)
@@ -223,7 +226,25 @@ def rank_program(g, core, T, topo):
         fill(["ONES"], T.ONES[:], 1.0)
         fill(["IND"], T.IND[:, 0:V], 64.0)
         fill(["IND"], T.IND[:, V:W], 0.0)
+        cp(["DJ"], ["DJ2"], T.DJ2[:, 0:16], T.DJ[:])
+        cp(["DJ"], ["DJ2"], T.DJ2[:, 16:32], T.DJ[:])
+        ts("v", ["k16"], ["RST"], T.RST[:], T.k16[:, 0:128], 0.0, float(1 << 26), OP.is_equal, OP.mult)
+        ts("v", ["RST"], ["RST"], T.RST[:], T.RST[:], -float(1 << 25), None, OP.add)
+        ts("v", ["k16"], ["NZ"], T.NZ[:], T.k16[:], 0.0, None, OP.is_gt)
+        cp(["IDN"], ["IDB"], T.IDB[:], T.IDN[:])
+        ts("v", ["IDN"], ["NIB"], T.NIB[:], T.IDN[:], -1.0, None, OP.mult)
+        fill(["VB"], T.VB[:], 4096.0 * V)
         act(["IDT"], ["HE"], T.HE[:], T.IDT[:], AF.Copy)
+
+    def closing_kin():
+        dma("y", ["HE"], [], "outs", T.yh[:], T.HE[0:128:16, 0:V])
+        act(XK, ["yxo"], T.yxo[:], T.X[:, 0:V], AF.Copy, scale=1.0 / 64, bias=-1.0 / 64)
+        dma("y", ["yxo"], [], "outs", T.yx[:], T.yxo[:])
+        act(KK, ["K16"], T.K16[:], T.K[:, 0:V], AF.Copy)
+        for q in range(4):
+            s, bk = slice(448 * q, 448 * q + 448), "B%d" % (4 + q)
+            op("p", ["K16", "KW"], [bk], lambda e: e.matmul(T[bk][0:8, 0:448], T.KW[:], T.K16[:, s], True, True))
+            act([bk], ["yko%d" % q], T.yko[0:8, s], T[bk][0:8, 0:448], AF.Copy)
 
     for t in range(T9):
         jub, last = t % 3 == 2, t == T9 - 1
@@ -233,15 +254,20 @@ def rank_program(g, core, T, topo):
             landing(prv, [Et], "e%d" % t)
             landing(prv, [Ht], "h%d" % t)
         yv, eu, hv = T.Yl[:, t, :], T.El[:, t, :], T.Hl[:, t, :]
+        yx = ["yx%d" % k for k in range(16)]
         for k in range(16):
             if k < KV:
                 cp([Yt], ["yx%d" % k], T.yexp[:, k:16 * P:16], yv)
             else:
                 act([Yt], ["yx%d" % k], T.yexp[:, k:16 * P:16], yv, AF.Copy)
-        cp(["K", Et], ["cU"], T.cU[:], T.K[:].indirect(eu))
-        act(["K", Et], ["c16"], T.c16[:], T.K[:].indirect(eu), AF.Copy)
+        kt, kk = (T.K, KK) if t else (T.kinb, ["kinb"])
+        cp(kk + [Et], ["cU"], T.cU[:], kt[:].indirect(eu))
+        act(kk + [Et], ["c16"], T.c16[:], kt[:].indirect(eu), AF.Copy)
         act(["c16", "gE"], ["Em0"], T.Em[:, :, 0:16], T.c16[:], AF.Copy, scale=c_("gE"))
         act(["c16", "gO"], ["Em1"], T.Em[:, :, 16:32], T.c16[:], AF.Copy, scale=c_("gO"))
+        act([Et], ["e17"], T.e17[:], eu, AF.Copy, bias=float(V))
+        act([Et], ["BEe"], T.BE[:, 16:32], eu, AF.Copy)
+        act(["c16", "even"], ["cm"], T.cm[:], T.c16[:], AF.Copy, scale=c_("even"))
 
         def kc(e):
             e.matmul(T.B2[:, 0:P], T.IDN[:], T.KKC[:], True, False)
@@ -251,64 +277,62 @@ def rank_program(g, core, T, topo):
                     e.matmul(T.B2[s, 16 * a:16 * a + 16], T.Em[s, a, :], T.OH[s, :], False, False)
             return e.matmul(T.B2[:, 0:P], T.IDN[:], T.KKC[:], False, True)
         op("p", ["Em0", "Em1", "OH", "IDN", "KKC"], ["B2"], kc)
-        for ch in range(4):
-            s, f = slice(4 * ch, 4 * ch + 4), slice(1024 * ch, 1024 * ch + 1024)
-            tt(["X", "cU"] + ["yx%d" % k for k in range(16)], ["DL%d" % ch], T.DL[:, f], T.X[:].indirect(T.cU[:, 64 * ch:64 * ch + 64]), T.yexp[:, f], OP.subtract)
+        for ch, (a0, na) in enumerate(CHUNKS):
+            s, f = slice(a0, a0 + na), slice(256 * a0, 256 * (a0 + na))
+            tt(XK + ["cU"] + yx, ["DL%d" % ch], T.DL[:, f], T.X[:].indirect(T.cU[:, 16 * a0:16 * (a0 + na)]), T.yexp[:, f], OP.subtract)
             act(["DL%d" % ch], ["AB%d" % ch], T.AB[:, s, :], T.DL[:, f], AF.Abs)
-            zb, o = ("B0", "B1")[ch // 2], 64 * (ch % 2)
+            zb, o = ("B0", "B1")[a0 // 8], 16 * (a0 % 8)
+            if ch == 0:
+                act([Yt], ["yqa"], T.yqa[:], yv, AF.Copy, scale=0.25, bias=-24.0)
+            elif ch == 1:
+                act(["yqa"], ["yqr"], T.yqr[:], T.yqa[:], AF.Copy, bias=MAGIC)
+            elif ch == 2:
+                act(["yqr"], ["yq"], T.yq[:], T.yqr[:], AF.Copy, bias=-MAGIC)
 
             def zsum(e):
                 for r in range(16):
-                    i = e.matmul(T[zb][:, o:o + 64], T.SEL[:, r, :], T.AB[:, s, 16 * r:16 * r + 16], r == 0, r == 15)
+                    i = e.matmul(T[zb][:, o:o + 16 * na], T.SEL[:, r, :], T.AB[:, s, 16 * r:16 * r + 16], r == 0, r == 15)
                 return i
             op("p", ["AB%d" % ch] + sel, [zb], zsum)
         if t == 0:
             late_constants()
-        act([Yt], ["yqa"], T.yqa[:], yv, AF.Copy, scale=0.25, bias=-24.0)
-        act(["c16", "even"], ["cm"], T.cm[:], T.c16[:], AF.Copy, scale=c_("even"))
-        cp([Et], ["ef"], T.ef[:], eu)
-        ts("v", [Et], ["e17"], T.e17[:], eu, float(V), None, OP.add)
         for h in range(2):
             zb, s, x = ("B0", "B1")[h], slice(8 * h, 8 * h + 8), str(h)
             z = T[zb][:, 0:128]
-            ts("v", [zb], ["s64" + x], T.s64[:, s, :], z, MAGIC, -MAGIC, OP.add, OP.add)
-            tt([zb, "s64" + x], ["low" + x], T.low[:, s, :], z, T.s64[:, s, :], OP.subtract)
-            ts("v", ["low" + x], ["mm" + x], T.mm[:, s, :], T.low[:, s, :], 4.0, 512.0, OP.is_lt, OP.mult)
-            tt(["mm" + x, "s64" + x], ["mm" + x], T.mm[:, s, :], T.mm[:, s, :], T.s64[:, s, :], OP.mult)
-            tt(["mm" + x, "B2"], ["key" + x], T.key[:, s, :], T.mm[:, s, :], T.B2[:, 128 * h:128 * h + 128], OP.add)
-            tt(["key" + x], ["t8" + x], T.t8[:, s, :], T.key[:, s, 0:8], T.key[:, s, 8:16], OP.min)
-            tt(["t8" + x], ["t4" + x], T.t4[:, s, :], T.t8[:, s, 0:4], T.t8[:, s, 4:8], OP.min)
-            tt(["t4" + x], ["t2" + x], T.t2[:, s, :], T.t4[:, s, 0:2], T.t4[:, s, 2:4], OP.min)
-            tt(["t2" + x], ["keyi" + x], T.keyi[:, s], T.t2[:, s, 0], T.t2[:, s, 1], OP.min)
-        ky = ["keyi0", "keyi1"]
-        ts("v", ky, ["Ff"], T.Ff[:], T.keyi[:], 32768.0, None, OP.is_ge)
-        ts("v", ky, ["bi"], T.bi[:], T.keyi[:], 2047, None, OP.bitwise_and)
-        tt(["Ff", "e17"], ["FE"], T.FE[:], T.Ff[:], T.e17[:], OP.mult)
-        cp(["bi"], ["bu"], T.bu[:], T.bi[:])
-        tt(["bi", "FE"], ["dk"], T.dk[:], T.bi[:], T.FE[:], OP.max)
-        tt(["BT%d" % u for u in range(7)] + ["dk", "POS"], ["C"], T.C[:], T.BT[:].indirect(T.dk[:]), T.POS[:], OP.add)
-        act(["IDT", "bu"], ["fr"], T.fr[:], T.IDT[:].indirect(T.bu[:]), AF.Copy)
-        for q in range(8):
-            if q < 5:
-                ts("v", ["C", "m1", "m2"], ["BD%d" % q], T.BDC[:, :, 16 * q:16 * q + 16], T.C[:], T.m1[:, q:q + 1], T.m2[:, q:q + 1], OP.mult, OP.add)
-            else:
-                act(["C", "m1", "m2"], ["BD%d" % q], T.BDC[:, :, 16 * q:16 * q + 16], T.C[:], AF.Identity, scale=T.m1[:, q:q + 1], bias=T.m2[:, q:q + 1])
-        for bank, q, aa in GRAM:
-            def gram(e):
-                o = 0
-                for a in aa:
-                    i = e.matmul(T[bank][:, o:o + 16 * a + 16], T.BDC[:, a, :], T.C[:, 0:16 * a + 16], True, True)
-                    o += 16 * a + 16
-                return i
-            op("p", ["C"] + ["BD%d" % i for i in range(8)], [bank], gram)
-        ts("v", ky, ["Of"], T.Of[:], T.keyi[:], 32768.0, None, OP.is_lt)
-        tt(["Ff", "DJ"], ["FD"], T.FD[:], T.Ff[:], T.DJ[:], OP.mult)
-        tt(["Of", "DJ"], ["OD"], T.OD[:], T.Of[:], T.DJ[:], OP.mult)
-        tt(["FD", "bi"], ["A1"], T.A1[:], T.bi[:], T.FD[:], OP.max)
-        tt(["OD", "ef"], ["A2"], T.A2[:], T.ef[:], T.OD[:], OP.max)
-        ts("v", ["yqa"], ["yq"], T.yq[:], T.yqa[:], MAGIC, -MAGIC, OP.add, OP.add)
-        tt(["X", "bu", "yq"], ["diff"], T.diff[:], T.X[:].indirect(T.bu[:]), T.yq[:], OP.subtract)
-        for bank, q, aa in GRAM:
+            sb = ("B4", "B5")[h]
+            poor, m = T[sb][:, 0:128], slice(128 * h, 128 * h + 128)
+            ts("v", [zb], ["s64" + x], T.s64[:, m], z, MAGIC, -MAGIC, OP.add, OP.add)
+            tt([zb, "s64" + x], ["low" + x], T.low[:, m], z, T.s64[:, m], OP.subtract)
+            ts("v", ["low" + x], [sb], poor, T.low[:, m], 4.0, 512.0, OP.is_lt, OP.mult)
+            tt([sb, "s64" + x], ["mm" + x], T.mm[:, m], T.s64[:, m], poor, OP.mult)
+            tt(["mm" + x, "B2"], ["key" + x], T.key[:, m], T.mm[:, m], T.B2[:, 128 * h:128 * h + 128], OP.add)
+            op("v", ["key" + x, "RST"], ["ks" + x], lambda e: e.tensor_tensor_scan(T.ks[:, m], T.RST[:], T.key[:, m], 0.0, OP.max, OP.min))
+            cp(["ks" + x], ["keyi" + x], T.keyi[:, s], T.ks[:, 128 * h + 15:128 * h + 128:16])
+            ts("v", ["keyi" + x], ["bi" + x], T.BE[:, s], T.keyi[:, s], 2047, None, OP.bitwise_and)
+            tt(["keyi" + x, "e17"], ["FE" + x], T.FE[:, s], T.keyi[:, s], T.e17[:, s], OP.min)
+            act(["bi" + x], ["bu" + x], T.bu[:, s], T.BE[:, s], AF.Copy)
+            tt(["bi" + x, "FE" + x], ["dk" + x], T.dk[:, s], T.BE[:, s], T.FE[:, s], OP.max)
+            tt(["BT%d" % u for u in range(7)] + ["dk" + x, "POS"], ["C" + x], T.C[:, m], T.BT[:].indirect(T.dk[:, s]), T.POS[:, m], OP.add)
+            for q in range(8):
+                if q < 5:
+                    ts("v", ["C" + x, "m1", "m2"], ["BD%d_%d" % (h, q)], T.BDC[:, s, 16 * q:16 * q + 16], T.C[:, m], T.m1[:, q:q + 1], T.m2[:, q:q + 1], OP.mult, OP.add)
+                else:
+                    act(["C" + x, "m1", "m2"], ["BD%d_%d" % (h, q)], T.BDC[:, s, 16 * q:16 * q + 16], T.C[:, m], AF.Identity, scale=T.m1[:, q:q + 1], bias=T.m2[:, q:q + 1])
+            for bank, _, aa in GRAM[h]:
+                def gram(e):
+                    o = 0
+                    for a in aa:
+                        i = e.matmul(T[bank][:, o:o + 16 * a + 16], T.BDC[:, a, :], T.C[:, 0:16 * a + 16], True, True)
+                        o += 16 * a + 16
+                    return i
+                op("p", ["C0", "C" + x] + ["BD%d_%d" % (h, q) for q in range(8)], [bank], gram)
+            if h:
+                act(["IDT", "bu0", "bu1"], ["fr"], T.fr[:], T.IDT[:].indirect(T.bu[:]), AF.Copy)
+        bus = ["bu0", "bu1"]
+        ts("v", ["keyi0", "keyi1"], ["nk"], T.keyi[:, 16:32], T.keyi[:, 0:16], -8.0, None, OP.mult)
+        tt(["keyi0", "keyi1", "nk", "DJ2"], ["A0"], T.A0[:], T.keyi[:], T.DJ2[:], OP.min)
+        tt(["A0", "bi0", "bi1", "BEe"], ["A12"], T.A12[:], T.A0[:], T.BE[:], OP.max)
+        for bank, q, aa in GRAM[0] + GRAM[1]:
             o = 0
             for a in aa:
                 z = T[bank][:, o:o + 16 * a + 16]
@@ -317,63 +341,70 @@ def rank_program(g, core, T, topo):
                     op("v", [bank], ["D%d" % a], lambda e: e.tensor_reduce(T.D[:, a:a + 1], z, AX.X, OP.max))
                 else:
                     act([bank, "BIAS"], ["D%d" % a, "junk%d" % a], T.junk[:, a, 0:16 * a + 16], z, AF.Relu, bias=T.BIAS[:, a:a + 1], accum_out=T.D[:, a:a + 1])
-        act(["K", "bu", "odd"], ["KF"], T.KF[:], T.K[:].indirect(T.bu[:]), AF.Copy, scale=c_("odd"))
         dv, ds = ["D%d" % a for a in range(NV)], ["D%d" % a for a in range(NV, 16)]
         tt(dv + ["BIAS"], dv, T.D[:, 0:NV], T.D[:, 0:NV], T.BIAS[:, 0:NV], OP.add)
         tt(dv + ds + ["DJ"], ["nd"], T.nd[:], T.D[:], T.DJ[:], OP.min)
-        tt(["nd", "A2"], ["o2"], T.o2[:], T.A2[:], T.nd[:], OP.max)
-        tt(["nd", "A1"], ["o1"], T.o1[:], T.A1[:], T.nd[:], OP.max)
-
-        def redeem_prices(k, out):
-            tt(["IND", "o1", Yt], ["YR"], T.YR[:], T.IND[:].indirect(T.o1[:]), yv, OP.add)
-            ts("v", ["YR"], [k], out, T.YR[:], 960.0, None, OP.min)
+        tt(["nd", "A12"], ["o2"], T.o2[:], T.A12[:, 16:32], T.nd[:], OP.max)
+        tt(["nd", "A12"], ["o1"], T.o1[:], T.A12[:, 0:16], T.nd[:], OP.max)
 
         def redeem_wealth():
-            tt(["diff", "o1", "ONES"], ["X"], T.X[:].indirect(T.o1[:]), T.diff[:], T.ONES[:], OP.max)
+            tt(["diff", "o1", "ONES"], XK, T.X[:].indirect(T.o1[:]), T.diff[:], T.ONES[:], OP.add)
 
         def kin_lines():
-            tt(["KF", "cm", "o2"], ["K"], T.K[:].indirect(T.o2[:]), T.KF[:], T.cm[:], OP.add)
+            tt(["KF", "cm", "o2"], KK, T.K[:].indirect(T.o2[:]), T.KF[:], T.cm[:], OP.add)
 
         def holders():
-            cp([Ht], ["hf"], T.hf[:], hv)
-            ts("v", ["o1"], ["R"], T.R[:], T.o1[:], float(V), None, OP.is_lt)
-            tt(["bi", "hf"], ["bh"], T.bh[:], T.bi[:], T.hf[:], OP.subtract)
-            tt(["R", "bh"], ["Rb"], T.Rb[:], T.R[:], T.bh[:], OP.mult)
+            tt(["uB", Ht], ["hx"], T.hx[:], T.uB[:], hv, OP.max)
+        act(["IND", "o1"], ["red"], T.red[:], T.IND[:].indirect(T.o1[:]), AF.Copy)
+
+        def raised(e):
+            e.matmul(T.B2[:, 0:P], T.IDB[:], yv, True, False)
+            return e.matmul(T.B2[:, 0:P], T.IDB[:], T.red[:], False, True)
+        op("p", ["IDB", Yt, "red"], ["B2"], raised)
+        act(XK + bus, ["xg"], T.xg[:], T.X[:].indirect(T.bu[:]), AF.Copy, bias=-1.0)
+
+        def paid(e):
+            e.matmul(T.B6[:, 0:P], T.IDB[:], T.xg[:], True, False)
+            return e.matmul(T.B6[:, 0:P], T.NIB[:], T.yq[:], False, True)
+        op("p", ["IDB", "NIB", "yq", "xg"], ["B6"], paid)
+        act(["B6"], ["diff"], T.diff[:], T.B6[:, 0:P], AF.Relu)
+        act(["o1"], ["uB"], T.uB[:], T.o1[:], AF.Relu, scale=-4096.0, bias=T.VB[:])
+        act(KK + ["bu0", "bu1", "odd"], ["KF"], T.KF[:], T.K[:].indirect(T.bu[:]), AF.Copy, scale=c_("odd"))
 
         cp(["fr", "o2"], ["HE"], T.HE[:].indirect(T.o2[:]), T.fr[:])
         Yk, Ek, Hk = "Yo%d" % t, "Eo%d" % t, "Ho%d" % t
         yo, eo, ho = T.Yo[:, t, :], T.Eo[:, t, :], T.Ho[:, t, :]
         if not jub:
-            redeem_prices(Yk, yo)
+            ts("v", ["B2"], [Yk], yo, T.B2[:, 0:P], 960.0, None, OP.min)
             send(nxt, [Yk], T.Yl[:, t + 1, :], yo, "y%d" % (t + 1))
         else:
-            redeem_prices("y1", T.prb[:])
             redeem_wealth()
+            ts("v", ["B2"], ["y1"], T.prb[:], T.B2[:, 0:P], 960.0, None, OP.min)
+            if last:
+                kin_lines()
+                closing_kin()
             wl, wk = ((T.W2, "W2"), (T.W1, "W1"), (T.Wo, "Wo"))[t // 3]
             cp([wk], ["wf"], T.wf[:], wl[:])
             ts("v", [wk], ["nw"], T.nw[:], wl[:], -1.0, 1.0, OP.mult, OP.add)
             holders()
-            tt(["Rb", "hf"], ["hn"], T.hn[:], T.Rb[:], T.hf[:], OP.add)
+            tt(["hx", "o1"], ["hn"], T.hn[:], T.hx[:], T.o1[:], OP.min)
             tt(["hn", "wf"], ["hw"], T.hw[:], T.hn[:], T.wf[:], OP.mult)
         tt(["HE", Et, "DELTA"], ["em"], T.em[:], T.HE[:].indirect(eu), T.DELTA[:], OP.mult)
-        tt(["em"], ["e8"], T.e8[:], T.em[:, 0:256:2], T.em[:, 1:256:2], OP.add)
-        tt(["e8"], ["e4"], T.e4[:], T.e8[:, 0:128:2], T.e8[:, 1:128:2], OP.add)
-        tt(["e4"], ["e2"], T.e2[:], T.e4[:, 0:64:2], T.e4[:, 1:64:2], OP.add)
+        op("v", ["em", "NZ"], ["es"], lambda e: e.tensor_tensor_scan(T.es[:], T.NZ[:], T.em[:], 0.0, OP.mult, OP.add))
         if not jub:
-            tt(["e2"], [Ek], eo, T.e2[:, 0:32:2], T.e2[:, 1:32:2], OP.add)
+            cp(["es"], [Ek], eo, T.es[:, 15:P:16])
             send(nxt, [Ek], T.El[:, t + 1, :], eo, "e%d" % (t + 1))
             redeem_wealth()
             kin_lines()
             holders()
-            tt(["Rb", "hf"], [Hk], ho, T.Rb[:], T.hf[:], OP.add)
+            tt(["hx", "o1"], [Hk], ho, T.hx[:], T.o1[:], OP.min)
             send(nxt, [Hk], T.Hl[:, t + 1, :], ho, "h%d" % (t + 1))
         else:
-            tt(["e2"], ["e1"], T.e1[:], T.e2[:, 0:32:2], T.e2[:, 1:32:2], OP.add)
-            tt(["e1", "nw"], ["e1n"], T.e1n[:], T.e1[:], T.nw[:], OP.mult)
+            tt(["es", "nw"], ["e1n"], T.e1n[:], T.es[:, 15:P:16], T.nw[:], OP.mult)
             tt(["e1n", "hw"], [Ek], eo, T.e1n[:], T.hw[:], OP.max)
             if not last:
                 send(nxt, [Ek], T.El[:, t + 1, :], eo, "e%d" % (t + 1))
-            tt(["X", Ek, "y1"], ["ti"], T.ti[:], T.X[:].indirect(eo), T.prb[:], OP.add)
+            tt(XK + [Ek, "y1"], ["ti"], T.ti[:], T.X[:].indirect(eo), T.prb[:], OP.add)
             ts("v", ["ti"], ["ti2"], T.ti2[:], T.ti[:], 7, None, OP.arith_shift_right)
             ts("v", ["ti2"], [Yk], yo, T.ti2[:], 64.0, None, OP.mult)
             if not last:
@@ -387,7 +418,12 @@ def rank_program(g, core, T, topo):
                     i = e.matmul(T.B2[:, 0:16], T.SELW[:, r, :], T.Yo[:, t, r:P:16], r == 0, r == 15)
                 return i
             op("p", ["SELW", Yk], ["B2"], wsum)
-            kin_lines()
+            if last:
+                cp(["IDT", Ek], ["ro0"], T.ro[:, 0, :], T.IDT[:].indirect(eo))
+                dma("y", ["ro0"], [], "outs", T.yo[:], T.ro[0:128:16, 0, :])
+                dma("y", ["yko%d" % q for q in range(4)], [], "outs", T.yk[:], T.yko[0:8, :])
+            else:
+                kin_lines()
             cp(["B2"], ["si"], T.si[:], T.B2[:, 0:16])
             ts("v", ["si"], ["si2"], T.si2[:], T.si[:], 6, 2047, OP.logical_shift_right, OP.bitwise_and)
             ts("v", ["si2"], ["si3"], T.si3[:], T.si2[:], float(V), -float(V), OP.is_ge, OP.mult)
@@ -395,22 +431,7 @@ def rank_program(g, core, T, topo):
             if not last:
                 send(nxt, [Hk], T.Hl[:, t + 1, :], ho, "h%d" % (t + 1))
 
-    dma("y", ["HE"], [], "outs", T.yh[:], T.HE[0:128:16, 0:V])
-    act(["X"], ["yxo"], T.yxo[:], T.X[:, 0:V], AF.Copy, scale=1.0 / 64, bias=-1.0 / 64)
-    dma("y", ["yxo"], [], "outs", T.yx[:], T.yxo[:])
-    cp(["K"], ["K16"], T.K16[:], T.K[:, 0:V])
-    for q in range(4):
-        s = slice(448 * q, 448 * q + 448)
-        bk = "B%d" % (4 + q)
-        op("p", ["K16", "KW"], [bk], lambda e: e.matmul(T[bk][0:8, 0:448], T.KW[:], T.K16[:, s], True, True))
-    act(["IDT", "Eo8"], ["ro0"], T.ro[:, 0, :], T.IDT[:].indirect(T.Eo[:, 8, :]), AF.Copy)
-    act(["IDT", "Ho8"], ["ro1"], T.ro[:, 1, :], T.IDT[:].indirect(T.Ho[:, 8, :]), AF.Copy)
-    for q in range(4):
-        s = slice(448 * q, 448 * q + 448)
-        bk = "B%d" % (4 + q)
-        cp([bk], ["yko"], T.yko[0:8, s], T[bk][0:8, 0:448])
-    dma("y", ["ro0"], [], "outs", T.yo[:], T.ro[0:128:16, 0, :])
+    cp(["IDT", "Ho8"], ["ro1"], T.ro[:, 1, :], T.IDT[:].indirect(T.Ho[:, 8, :]))
     dma("y", ["ro1"], [], "outs", T.yt[:], T.ro[0:128:16, 1, :])
-    dma("y", ["yko"], [], "outs", T.yk[:], T.yko[0:8, :])
     for sem in ("v", "s", "p", "g", "lsem", "outs"):
         g.wait_ge(T.sem[sem], cnt[sem])

@@ -5,8 +5,18 @@ BIG = float(1 << 20)
 MAGIC = 1.5 * (1 << 23) * 64
 KV = 11
 CHUNKS = [(0, 4), (4, 4), (8, 4), (12, 4)]
-GRAM = [[("B3", "v", (7, 6, 5)), ("B6", "v", (4, 3, 2, 1, 0))], [("B7", "s", (15, 14)), ("B5", "v", (11, 10, 8)), ("B0", "s", (13, 12)), ("B4", "v", (9,))]]
-NV = 12
+MA = (5, 6)
+GRAM = [[("B3", "v", (7, 6, 5, 4, 1, 0))], [("B7", "s", (15, 14)), ("B5", "v", (11, 10, 3, 2)), ("B0", "s", (13,)), ("B4", "v", (12, 9, 8))]]
+SEG, BASE = {}, {}
+_o = 0
+for _b, _q, _aa in GRAM[0] + GRAM[1]:
+    if _q == "v":
+        BASE[_b] = _o
+        for _a in _aa:
+            SEG[_a] = (_o, _o + 16 * _a + 15)
+            _o += 16 * _a + 16
+NSC = _o
+SA = [_a for _a in range(16) if _a not in SEG]
 
 F32, BF16, F16, I32, U16 = "float32", "bfloat16", "float16", "int32", "uint16"
 SCRATCH = {"B%d" % i: ("psum", [128, 512], F32) for i in range(8)}
@@ -16,17 +26,19 @@ for _n, _s, _d in [
         ("Yl", [9, P], BF16), ("Yo", [9, P], BF16), ("El", [9, 16], U16), ("Eo", [9, 16], U16), ("Hl", [9, 16], U16), ("Ho", [9, 16], U16),
         ("Wo", [16], U16), ("W1", [16], U16), ("W2", [16], U16),
         ("yexp", [16 * P], BF16), ("cU", [P], U16), ("c16", [P], F16), ("Em", [16, 32], F16), ("cm", [P], F32),
-        ("DL", [16 * P], F16), ("AB", [16, P], F16), ("s64", [P], F32), ("low", [P], F32), ("mm", [P], F32), ("key", [P], F32),
+        ("DL", [16 * P], F16), ("AB", [16, P], F16), ("s64", [P], F32), ("mm", [P], F32), ("key", [P], F32),
         ("ks", [P], F32), ("RST", [128], F32), ("keyi", [32], I32), ("BE", [32], I32), ("FE", [16], F32), ("DJ2", [32], F32), ("A0", [32], F32), ("A12", [32], F32),
         ("dk", [16], U16), ("bu", [16], U16), ("e17", [16], F32), ("VB", [1], F32), ("uB", [16], F32), ("hx", [16], F32),
-        ("C", [P], BF16), ("BDC", [16, 128], BF16), ("D", [16], F32), ("junk", [16, P], BF16), ("nd", [16], F32), ("o1", [16], U16), ("o2", [16], U16),
+        ("C", [P], BF16), ("BDC", [16, 128], BF16), ("D", [32], F32), ("junk", [16, P], BF16), ("nd", [32], F32), ("o12", [32], U16),
+        ("SC", [NSC + 16], F32), ("RSTG", [NSC], F32), ("ENDS", [16], F32), ("ENDM", [16], F32), ("ENDC", [1], F32), ("ENDL", [2], U16), ("BIAS2", [32], F32),
+        ("M3", [64], F16), ("OHS", [16], F16),
         ("fr", [P], F32), ("KF", [P], F32), ("yqa", [P], F32), ("yqr", [P], F32), ("yq", [P], BF16), ("xg", [P], BF16), ("diff", [P], F32), ("red", [P], BF16), ("IDB", [128], BF16), ("NIB", [128], BF16),
         ("em", [P], F32), ("es", [P], F32), ("NZ", [P], F32), ("e1n", [16], F32),
         ("hn", [16], F32), ("hw", [16], F32), ("wf", [16], F32), ("nw", [16], F32),
         ("ti", [P], I32), ("ti2", [P], I32), ("si", [16], I32), ("si2", [16], I32), ("si3", [16], F32),
         ("pidx", [1], I32), ("cols", [32], F32), ("ints", [8], I32), ("i8", [8], F32), ("GM", [8], F32), ("m1", [8], F32), ("m2", [8], F32),
         ("k16", [P], F32), ("DELTA", [P], F32), ("OH", [16], F16), ("SEL", [16, 128], F16), ("SELW", [16, 128], BF16), ("IDN", [128], F16), ("KKC", [P], F16),
-        ("i128", [128], F32), ("POS", [P], F32), ("PJ", [16], F32), ("BIAS", [16], F32), ("DJ", [16], F32), ("ONES", [P], F32),
+        ("i128", [128], F32), ("POS", [P], F32), ("PJ", [32], F32), ("BIAS", [16], F32), ("DJ", [16], F32), ("ONES", [P], F32),
         ("WI", [520], F32), ("WB", [520], I32), ("WC", [520], I32), ("LOWC", [512], BF16), ("HIGH", [8], F32), ("KW", [8], F16),
         ("K16", [V], F16), ("yxo", [V], BF16), ("yko", [V], F32), ("ro", [2, P], F32)]:
     SCRATCH[_n] = ("sbuf", [128] + _s, _d)
@@ -142,10 +154,20 @@ def rank_program(g, core, T, topo):
     iota("k16", T.k16[:], [[0, 16], [1, 16]], 0, 0)
     iota("WI", T.WI[:, 0:512], [[1, 512]], 0, 0)
     iota("WI2", T.WI[:, 512:520], [[512, 8]], 0, 0)
-    iota("PJ", T.PJ[:], [[16, 16]], 0, 0)
+    iota("PJ", T.PJ[:], [[0, 2], [16, 16]], 0, 0)
     iota("i128", T.i128[:], [[1, 128]], 0, 0)
     iota("POS", T.POS[:], [[1, P]], 0, 0)
+    iota("Xt", T.X[:, V:W], [[0, W - V]], 1, 0)
+    iota("Kt", T.K[:, V:W], [[0, W - V]], 0, 0)
+    iota("ONES", T.ONES[:], [[0, P]], 1, 0)
+    iota("RSTG", T.RSTG[:], [[0, NSC]], (1 << 24) - 1, 0)
+    iota("SC", T.SC[:, NSC:NSC + 16], [[0, 16]], 0, 0)
+    for a in range(16):
+        iota("ENDS%d" % a, T.ENDS[:, a:a + 1], [[0, 1]], SEG[a][1] if a in SEG else NSC + a, 0)
+        if a in SEG:
+            iota("RSTG", T.RSTG[:, SEG[a][0]:SEG[a][0] + 1], [[0, 1]], 1 - (1 << 24), 0)
     iota("IDT", T.IDT[:], [[1, W]], 0, 0)
+    iota("HE", T.HE[:], [[1, W]], 0, 0)
 
     col = {}
 
@@ -186,17 +208,25 @@ def rank_program(g, core, T, topo):
     ts("v", ["i8", "gF"], ["GM"], T.GM[:], T.i8[:], c_("gF"), None, OP.is_equal)
     ts("v", ["k16", "iF"], ["OH"], T.OH[:], T.k16[:, 0:16], c_("iF"), None, OP.is_equal)
     ts("v", ["k16", "iF"], ["DELTA"], T.DELTA[:], T.k16[:], c_("iF"), None, OP.is_equal)
-    ts("v", ["k16"], ["KKC"], T.KKC[:], T.k16[:], 1024.0, -16384.0, OP.mult, OP.add)
+    ts("v", ["k16"], ["KKC"], T.KKC[:], T.k16[:], 2.0, -32.0, OP.mult, OP.add)
     ts("v", ["i128", "pF"], ["IDN"], T.IDN[:], T.i128[:], c_("pF"), None, OP.is_equal)
     sel = ["SEL%d" % r for r in range(16)]
     fill(sel, T.SEL[:], 0.0)
     for r in range(16):
-        cp(["GM"], ["SEL%d" % r], T.SEL[:, r, r:128:16], T.GM[:])
+        if r < 8:
+            cp(["GM"], ["SEL%d" % r], T.SEL[:, r, r:128:16], T.GM[:])
+        else:
+            act(["GM"], ["SEL%d" % r], T.SEL[:, r, r:128:16], T.GM[:], AF.Copy)
+    fill(["M3"], T.M3[:], -3.0)
+    ts("v", ["OH"], ["OHS"], T.OHS[:], T.OH[:], 1.0 / 512, None, OP.mult)
+    ts("v", ["WI", "pw", "ph"], ["WB"], T.WB[:, 0:512], T.WI[:, 0:512], c_("pw"), c_("ph"), OP.mult, OP.add)
+    ts("v", ["WI2", "pw", "ph"], ["WB2"], T.WB[:, 512:520], T.WI[:, 512:520], c_("pw"), c_("ph"), OP.mult, OP.add)
+    ts("v", ["WB", "WB2"], ["WC"], T.WC[:], T.WB[:], 1, None, OP.bitwise_and)
+    ts("v", ["WC", "l9d", "l9n"], ["LOWC"], T.LOWC[:], T.WC[:, 0:512], c_("l9d"), c_("l9n"), OP.mult, OP.add)
+    ts("v", ["WC", "h3d", "h3n"], ["HIGH"], T.HIGH[:], T.WC[:, 512:520], c_("h3d"), c_("h3n"), OP.mult, OP.add)
 
     cp(["ownb"], ["El0"], T.El[:, 0, :], T.ownb[:])
     ts("v", ["prb"], ["Yl0"], T.Yl[:, 0, :], T.prb[:], 64.0, None, OP.mult)
-    fill(["Kt"], T.K[:, V:W], 0.0)
-    fill(["Xt"], T.X[:, V:W], 1.0)
     ts("v", ["xb"], ["Xa"], T.X[:, 0:768], T.xb[:, 0:768], 64.0, 1.0, OP.mult, OP.add)
     act(["xb"], ["Xb"], T.X[:, 768:V], T.xb[:, 768:V], AF.Copy, scale=64.0, bias=1.0)
     XK, KK = ["Xa", "Xb", "Xt"], ["K", "Kt"]
@@ -208,42 +238,46 @@ def rank_program(g, core, T, topo):
     cp(["holdb"], ["Hl0"], T.Hl[:, 0, :], T.holdb[:])
 
     def late_constants():
-        cp(["kinb"], ["K"], T.K[:, 0:V], T.kinb[:])
-        ts("v", ["WI", "pw", "ph"], ["WB"], T.WB[:, 0:512], T.WI[:, 0:512], c_("pw"), c_("ph"), OP.mult, OP.add)
-        ts("v", ["WI2", "pw", "ph"], ["WB2"], T.WB[:, 512:520], T.WI[:, 512:520], c_("pw"), c_("ph"), OP.mult, OP.add)
-        ts("v", ["WB", "WB2"], ["WC"], T.WC[:], T.WB[:], 1, None, OP.bitwise_and)
-        ts("v", ["WC", "l9d", "l9n"], ["LOWC"], T.LOWC[:], T.WC[:, 0:512], c_("l9d"), c_("l9n"), OP.mult, OP.add)
-        ts("v", ["WC", "h3d", "h3n"], ["HIGH"], T.HIGH[:], T.WC[:, 512:520], c_("h3d"), c_("h3n"), OP.mult, OP.add)
         for u in range(7):
-            ts("v", ["LOWC", "HIGH"], ["BT%d" % u], T.BT[:, 512 * u:512 * u + 512], T.LOWC[:], T.HIGH[:, u:u + 1], None, OP.add)
+            o = T.BT[:, 512 * u:512 * u + 512]
+            if u < 5:
+                ts("v", ["LOWC", "HIGH"], ["BT%d" % u], o, T.LOWC[:], T.HIGH[:, u:u + 1], None, OP.add)
+            else:
+                act(["LOWC", "HIGH"], ["BT%d" % u], o, T.LOWC[:], AF.Identity, bias=T.HIGH[:, u:u + 1])
+        act(["kinb"], ["K"], T.K[:, 0:V], T.kinb[:], AF.Copy)
         ts("v", ["POS", "q12"], ["POS"], T.POS[:], T.POS[:], c_("q12"), None, OP.mult)
         ts("v", ["GM", "s12"], ["m1"], T.m1[:], T.GM[:], c_("s12"), None, OP.mult)
         ts("v", ["GM", "b12"], ["m2"], T.m2[:], T.GM[:], c_("b12"), None, OP.mult)
         ts("v", ["GM", "i1"], ["KW"], T.KW[:], T.GM[:], c_("i1"), None, OP.mult)
         ts("v", ["PJ", "iF"], ["PJ"], T.PJ[:], T.PJ[:], c_("iF"), None, OP.add)
-        ts("v", ["PJ"], ["BIAS"], T.BIAS[:], T.PJ[:], BIG / 256, -12.0 * BIG, OP.mult, OP.add)
-        ts("v", ["PJ"], ["DJ"], T.DJ[:], T.PJ[:], float(V), None, OP.add)
-        fill(["ONES"], T.ONES[:], 1.0)
-        fill(["IND"], T.IND[:, 0:V], 64.0)
-        fill(["IND"], T.IND[:, V:W], 0.0)
-        cp(["DJ"], ["DJ2"], T.DJ2[:, 0:16], T.DJ[:])
-        cp(["DJ"], ["DJ2"], T.DJ2[:, 16:32], T.DJ[:])
+        ts("v", ["PJ"], ["BIAS"], T.BIAS[:], T.PJ[:, 0:16], BIG / 256, -12.0 * BIG, OP.mult, OP.add)
+        ts("v", ["PJ"], ["DJ2"], T.DJ2[:], T.PJ[:], float(V), None, OP.add)
+        ts("v", ["PJ"], ["BIAS2"], T.BIAS2[:], T.PJ[:], BIG / 256, -12.0 * BIG, OP.mult, OP.add)
+        for a in SA:
+            fill(["BIAS2"], T.BIAS2[:, a:32:16], 0.0)
+        tt(["OH"] + ["ENDS%d" % a for a in range(16)], ["ENDM"], T.ENDM[:], T.ENDS[:], T.OH[:], OP.mult)
+        op("v", ["ENDM"], ["ENDC"], lambda e: e.tensor_reduce(T.ENDC[:], T.ENDM[:], AX.X, OP.add))
+        for i in range(2):
+            cp(["ENDC"], ["ENDL%d" % i], T.ENDL[:, i:i + 1], T.ENDC[:])
+        fill(["INDa"], T.IND[:, 0:V], 64.0)
+        fill(["INDb"], T.IND[:, V:W], 0.0)
         ts("v", ["k16"], ["RST"], T.RST[:], T.k16[:, 0:128], 0.0, float(1 << 26), OP.is_equal, OP.mult)
         ts("v", ["RST"], ["RST"], T.RST[:], T.RST[:], -float(1 << 25), None, OP.add)
         ts("v", ["k16"], ["NZ"], T.NZ[:], T.k16[:], 0.0, None, OP.is_gt)
         cp(["IDN"], ["IDB"], T.IDB[:], T.IDN[:])
         ts("v", ["IDN"], ["NIB"], T.NIB[:], T.IDN[:], -1.0, None, OP.mult)
         fill(["VB"], T.VB[:], 4096.0 * V)
-        act(["IDT"], ["HE"], T.HE[:], T.IDT[:], AF.Copy)
 
     def closing_kin():
         dma("y", ["HE"], [], "outs", T.yh[:], T.HE[0:128:16, 0:V])
-        act(XK, ["yxo"], T.yxo[:], T.X[:, 0:V], AF.Copy, scale=1.0 / 64, bias=-1.0 / 64)
-        dma("y", ["yxo"], [], "outs", T.yx[:], T.yxo[:])
-        act(KK, ["K16"], T.K16[:], T.K[:, 0:V], AF.Copy)
         for q in range(4):
             s, bk = slice(448 * q, 448 * q + 448), "B%d" % (4 + q)
-            op("p", ["K16", "KW"], [bk], lambda e: e.matmul(T[bk][0:8, 0:448], T.KW[:], T.K16[:, s], True, True))
+            act(KK, ["K16_%d" % q], T.K16[:, s], T.K[:, s], AF.Copy)
+            op("p", ["K16_%d" % q, "KW"], [bk], lambda e: e.matmul(T[bk][0:8, 0:448], T.KW[:], T.K16[:, s], True, True))
+        act(XK, ["yxo"], T.yxo[:], T.X[:, 0:V], AF.Copy, scale=1.0 / 64, bias=-1.0 / 64)
+        dma("y", ["yxo"], [], "outs", T.yx[:], T.yxo[:])
+        for q in range(2):
+            s, bk = slice(448 * q, 448 * q + 448), "B%d" % (4 + q)
             act([bk], ["yko%d" % q], T.yko[0:8, s], T[bk][0:8, 0:448], AF.Copy)
 
     for t in range(T9):
@@ -274,47 +308,52 @@ def rank_program(g, core, T, topo):
             for A in range(4):
                 s = slice(32 * A, 32 * A + 32)
                 for a in range(16):
-                    e.matmul(T.B2[s, 16 * a:16 * a + 16], T.Em[s, a, :], T.OH[s, :], False, False)
+                    e.matmul(T.B2[s, 16 * a:16 * a + 16], T.Em[s, a, :], T.OHS[s, :], False, False)
             return e.matmul(T.B2[:, 0:P], T.IDN[:], T.KKC[:], False, True)
-        op("p", ["Em0", "Em1", "OH", "IDN", "KKC"], ["B2"], kc)
+        op("p", ["Em0", "Em1", "OHS", "IDN", "KKC"], ["B2"], kc)
         for ch, (a0, na) in enumerate(CHUNKS):
             s, f = slice(a0, a0 + na), slice(256 * a0, 256 * (a0 + na))
             tt(XK + ["cU"] + yx, ["DL%d" % ch], T.DL[:, f], T.X[:].indirect(T.cU[:, 16 * a0:16 * (a0 + na)]), T.yexp[:, f], OP.subtract)
             act(["DL%d" % ch], ["AB%d" % ch], T.AB[:, s, :], T.DL[:, f], AF.Abs)
             zb, o = ("B0", "B1")[a0 // 8], 16 * (a0 % 8)
-            if ch == 0:
-                act([Yt], ["yqa"], T.yqa[:], yv, AF.Copy, scale=0.25, bias=-24.0)
-            elif ch == 1:
-                act(["yqa"], ["yqr"], T.yqr[:], T.yqa[:], AF.Copy, bias=MAGIC)
-            elif ch == 2:
-                act(["yqr"], ["yq"], T.yq[:], T.yqr[:], AF.Copy, bias=-MAGIC)
 
             def zsum(e):
+                e.matmul(T[zb][:, o:o + 16 * na], T.IDN[:], T.M3[:, 0:16 * na], True, False)
                 for r in range(16):
-                    i = e.matmul(T[zb][:, o:o + 16 * na], T.SEL[:, r, :], T.AB[:, s, 16 * r:16 * r + 16], r == 0, r == 15)
+                    i = e.matmul(T[zb][:, o:o + 16 * na], T.SEL[:, r, :], T.AB[:, s, 16 * r:16 * r + 16], False, r == 15)
                 return i
-            op("p", ["AB%d" % ch] + sel, [zb], zsum)
+            op("p", ["AB%d" % ch, "M3", "IDN"] + sel, [zb], zsum)
         if t == 0:
             late_constants()
+
+        def quarter():
+            act([Yt], ["yqa"], T.yqa[:], yv, AF.Copy, scale=0.25, bias=-24.0)
+            act(["yqa"], ["yqr"], T.yqr[:], T.yqa[:], AF.Copy, bias=MAGIC)
+            act(["yqr"], ["yq"], T.yq[:], T.yqr[:], AF.Copy, bias=-MAGIC)
+        if jub:
+            wl, wk = ((T.W2, "W2"), (T.W1, "W1"), (T.Wo, "Wo"))[t // 3]
+            act([wk], ["wf"], T.wf[:], wl[:], AF.Copy)
+            act([wk], ["nw"], T.nw[:], wl[:], AF.Copy, scale=-1.0, bias=1.0)
         for h in range(2):
             zb, s, x = ("B0", "B1")[h], slice(8 * h, 8 * h + 8), str(h)
             z = T[zb][:, 0:128]
             sb = ("B4", "B5")[h]
             poor, m = T[sb][:, 0:128], slice(128 * h, 128 * h + 128)
             ts("v", [zb], ["s64" + x], T.s64[:, m], z, MAGIC, -MAGIC, OP.add, OP.add)
-            tt([zb, "s64" + x], ["low" + x], T.low[:, m], z, T.s64[:, m], OP.subtract)
-            ts("v", ["low" + x], [sb], poor, T.low[:, m], 4.0, 512.0, OP.is_lt, OP.mult)
+            tt([zb, "s64" + x], [sb], poor, z, T.s64[:, m], OP.is_lt)
             tt([sb, "s64" + x], ["mm" + x], T.mm[:, m], T.s64[:, m], poor, OP.mult)
             tt(["mm" + x, "B2"], ["key" + x], T.key[:, m], T.mm[:, m], T.B2[:, 128 * h:128 * h + 128], OP.add)
             op("v", ["key" + x, "RST"], ["ks" + x], lambda e: e.tensor_tensor_scan(T.ks[:, m], T.RST[:], T.key[:, m], 0.0, OP.max, OP.min))
-            cp(["ks" + x], ["keyi" + x], T.keyi[:, s], T.ks[:, 128 * h + 15:128 * h + 128:16])
+            ts("v", ["ks" + x], ["keyi" + x], T.keyi[:, s], T.ks[:, 128 * h + 15:128 * h + 128:16], 512.0, None, OP.mult)
             ts("v", ["keyi" + x], ["bi" + x], T.BE[:, s], T.keyi[:, s], 2047, None, OP.bitwise_and)
             tt(["keyi" + x, "e17"], ["FE" + x], T.FE[:, s], T.keyi[:, s], T.e17[:, s], OP.min)
             act(["bi" + x], ["bu" + x], T.bu[:, s], T.BE[:, s], AF.Copy)
+            if h:
+                act(["keyi0", "keyi1"], ["nk"], T.keyi[:, 16:32], T.keyi[:, 0:16], AF.Copy, scale=-8.0)
             tt(["bi" + x, "FE" + x], ["dk" + x], T.dk[:, s], T.BE[:, s], T.FE[:, s], OP.max)
             tt(["BT%d" % u for u in range(7)] + ["dk" + x, "POS"], ["C" + x], T.C[:, m], T.BT[:].indirect(T.dk[:, s]), T.POS[:, m], OP.add)
             for q in range(8):
-                if q < 5:
+                if q < MA[h]:
                     ts("v", ["C" + x, "m1", "m2"], ["BD%d_%d" % (h, q)], T.BDC[:, s, 16 * q:16 * q + 16], T.C[:, m], T.m1[:, q:q + 1], T.m2[:, q:q + 1], OP.mult, OP.add)
                 else:
                     act(["C" + x, "m1", "m2"], ["BD%d_%d" % (h, q)], T.BDC[:, s, 16 * q:16 * q + 16], T.C[:, m], AF.Identity, scale=T.m1[:, q:q + 1], bias=T.m2[:, q:q + 1])
@@ -326,52 +365,65 @@ def rank_program(g, core, T, topo):
                         o += 16 * a + 16
                     return i
                 op("p", ["C0", "C" + x] + ["BD%d_%d" % (h, q) for q in range(8)], [bank], gram)
+            if h == 0 and jub:
+                quarter()
             if h:
                 act(["IDT", "bu0", "bu1"], ["fr"], T.fr[:], T.IDT[:].indirect(T.bu[:]), AF.Copy)
         bus = ["bu0", "bu1"]
-        ts("v", ["keyi0", "keyi1"], ["nk"], T.keyi[:, 16:32], T.keyi[:, 0:16], -8.0, None, OP.mult)
         tt(["keyi0", "keyi1", "nk", "DJ2"], ["A0"], T.A0[:], T.keyi[:], T.DJ2[:], OP.min)
         tt(["A0", "bi0", "bi1", "BEe"], ["A12"], T.A12[:], T.A0[:], T.BE[:], OP.max)
         for bank, q, aa in GRAM[0] + GRAM[1]:
-            o = 0
+            o, w = 0, sum(16 * a + 16 for a in aa)
+            if q == "v":
+                z, b = T[bank][:, 0:w], BASE[bank]
+                op("v", [bank, "RSTG", "SC"], ["SC" + bank], lambda e: e.tensor_tensor_scan(T.SC[:, b:b + w], T.RSTG[:, b:b + w], z, 0.0, OP.min, OP.max))
+                continue
             for a in aa:
                 z = T[bank][:, o:o + 16 * a + 16]
                 o += 16 * a + 16
-                if q == "v":
-                    op("v", [bank], ["D%d" % a], lambda e: e.tensor_reduce(T.D[:, a:a + 1], z, AX.X, OP.max))
-                else:
-                    act([bank, "BIAS"], ["D%d" % a, "junk%d" % a], T.junk[:, a, 0:16 * a + 16], z, AF.Relu, bias=T.BIAS[:, a:a + 1], accum_out=T.D[:, a:a + 1])
-        dv, ds = ["D%d" % a for a in range(NV)], ["D%d" % a for a in range(NV, 16)]
-        tt(dv + ["BIAS"], dv, T.D[:, 0:NV], T.D[:, 0:NV], T.BIAS[:, 0:NV], OP.add)
-        tt(dv + ds + ["DJ"], ["nd"], T.nd[:], T.D[:], T.DJ[:], OP.min)
-        tt(["nd", "A12"], ["o2"], T.o2[:], T.A12[:, 16:32], T.nd[:], OP.max)
-        tt(["nd", "A12"], ["o1"], T.o1[:], T.A12[:, 0:16], T.nd[:], OP.max)
+                act([bank, "BIAS", "SC"], ["SC%d" % a, "junk%d" % a], T.junk[:, a, 0:16 * a + 16], z, AF.Relu, bias=T.BIAS[:, a:a + 1], accum_out=T.SC[:, NSC + a:NSC + a + 1])
+        tt(["SC"] + ["SC" + b for b in BASE] + ["SC%d" % a for a in SA] + ["ENDL0", "ENDL1", "BIAS2"], ["D"], T.D[:], T.SC[:].indirect(T.ENDL[:]), T.BIAS2[:], OP.add)
+        tt(["D", "DJ2"], ["nd"], T.nd[:], T.D[:], T.DJ2[:], OP.min)
+        tt(["nd", "A12"], ["o1", "o2"], T.o12[:], T.A12[:], T.nd[:], OP.max)
+        o1, o2 = T.o12[:, 0:16], T.o12[:, 16:32]
 
         def redeem_wealth():
-            tt(["diff", "o1", "ONES"], XK, T.X[:].indirect(T.o1[:]), T.diff[:], T.ONES[:], OP.add)
+            tt(["diff", "o1", "ONES"], XK, T.X[:].indirect(o1), T.diff[:], T.ONES[:], OP.add)
 
         def kin_lines():
-            tt(["KF", "cm", "o2"], KK, T.K[:].indirect(T.o2[:]), T.KF[:], T.cm[:], OP.add)
+            tt(["KF", "cm", "o2"], KK, T.K[:].indirect(o2), T.KF[:], T.cm[:], OP.add)
 
         def holders():
             tt(["uB", Ht], ["hx"], T.hx[:], T.uB[:], hv, OP.max)
-        act(["IND", "o1"], ["red"], T.red[:], T.IND[:].indirect(T.o1[:]), AF.Copy)
+        def kin_of_kin():
+            act(kk + ["bu0", "bu1", "odd"], ["KF"], T.KF[:], kt[:].indirect(T.bu[:]), AF.Copy, scale=c_("odd"))
 
-        def raised(e):
-            e.matmul(T.B2[:, 0:P], T.IDB[:], yv, True, False)
-            return e.matmul(T.B2[:, 0:P], T.IDB[:], T.red[:], False, True)
-        op("p", ["IDB", Yt, "red"], ["B2"], raised)
-        act(XK + bus, ["xg"], T.xg[:], T.X[:].indirect(T.bu[:]), AF.Copy, bias=-1.0)
+        def wealth_of_kin():
+            act(XK + bus, ["xg"], T.xg[:], T.X[:].indirect(T.bu[:]), AF.Copy, bias=-1.0)
 
-        def paid(e):
-            e.matmul(T.B6[:, 0:P], T.IDB[:], T.xg[:], True, False)
-            return e.matmul(T.B6[:, 0:P], T.NIB[:], T.yq[:], False, True)
-        op("p", ["IDB", "NIB", "yq", "xg"], ["B6"], paid)
-        act(["B6"], ["diff"], T.diff[:], T.B6[:, 0:P], AF.Relu)
-        act(["o1"], ["uB"], T.uB[:], T.o1[:], AF.Relu, scale=-4096.0, bias=T.VB[:])
-        act(KK + ["bu0", "bu1", "odd"], ["KF"], T.KF[:], T.K[:].indirect(T.bu[:]), AF.Copy, scale=c_("odd"))
+        def paid():
+            op("p", ["IDB", "NIB", "yq", "xg"], ["B6"], lambda e: (e.matmul(T.B6[:, 0:P], T.IDB[:], T.xg[:], True, False), e.matmul(T.B6[:, 0:P], T.NIB[:], T.yq[:], False, True))[1])
+            act(["B6"], ["diff"], T.diff[:], T.B6[:, 0:P], AF.Relu)
 
-        cp(["fr", "o2"], ["HE"], T.HE[:].indirect(T.o2[:]), T.fr[:])
+        def raised():
+            act(["INDa", "INDb", "o1"], ["red"], T.red[:], T.IND[:].indirect(o1), AF.Copy)
+            op("p", ["IDB", "red"], ["B2"], lambda e: e.matmul(T.B2[:, 0:P], T.IDB[:], T.red[:], False, True))
+        op("p", ["IDB", Yt], ["B2"], lambda e: e.matmul(T.B2[:, 0:P], T.IDB[:], yv, True, False))
+        if jub:
+            wealth_of_kin()
+            paid()
+            raised()
+            act(["o1"], ["uB"], T.uB[:], o1, AF.Relu, scale=-4096.0, bias=T.VB[:])
+            kin_of_kin()
+        else:
+            kin_of_kin()
+            raised()
+            act(["o1"], ["uB"], T.uB[:], o1, AF.Relu, scale=-4096.0, bias=T.VB[:])
+            wealth_of_kin()
+            quarter()
+            paid()
+
+        cp(["fr", "o2"], ["HE"], T.HE[:].indirect(o2), T.fr[:])
         Yk, Ek, Hk = "Yo%d" % t, "Eo%d" % t, "Ho%d" % t
         yo, eo, ho = T.Yo[:, t, :], T.Eo[:, t, :], T.Ho[:, t, :]
         if not jub:
@@ -383,21 +435,18 @@ def rank_program(g, core, T, topo):
             if last:
                 kin_lines()
                 closing_kin()
-            wl, wk = ((T.W2, "W2"), (T.W1, "W1"), (T.Wo, "Wo"))[t // 3]
-            cp([wk], ["wf"], T.wf[:], wl[:])
-            ts("v", [wk], ["nw"], T.nw[:], wl[:], -1.0, 1.0, OP.mult, OP.add)
             holders()
-            tt(["hx", "o1"], ["hn"], T.hn[:], T.hx[:], T.o1[:], OP.min)
+            tt(["hx", "o1"], ["hn"], T.hn[:], T.hx[:], o1, OP.min)
             tt(["hn", "wf"], ["hw"], T.hw[:], T.hn[:], T.wf[:], OP.mult)
         tt(["HE", Et, "DELTA"], ["em"], T.em[:], T.HE[:].indirect(eu), T.DELTA[:], OP.mult)
         op("v", ["em", "NZ"], ["es"], lambda e: e.tensor_tensor_scan(T.es[:], T.NZ[:], T.em[:], 0.0, OP.mult, OP.add))
         if not jub:
             cp(["es"], [Ek], eo, T.es[:, 15:P:16])
             send(nxt, [Ek], T.El[:, t + 1, :], eo, "e%d" % (t + 1))
-            redeem_wealth()
             kin_lines()
+            redeem_wealth()
             holders()
-            tt(["hx", "o1"], [Hk], ho, T.hx[:], T.o1[:], OP.min)
+            tt(["hx", "o1"], [Hk], ho, T.hx[:], o1, OP.min)
             send(nxt, [Hk], T.Hl[:, t + 1, :], ho, "h%d" % (t + 1))
         else:
             tt(["es", "nw"], ["e1n"], T.e1n[:], T.es[:, 15:P:16], T.nw[:], OP.mult)
@@ -421,6 +470,8 @@ def rank_program(g, core, T, topo):
             if last:
                 cp(["IDT", Ek], ["ro0"], T.ro[:, 0, :], T.IDT[:].indirect(eo))
                 dma("y", ["ro0"], [], "outs", T.yo[:], T.ro[0:128:16, 0, :])
+                for q in range(2, 4):
+                    cp(["B%d" % (4 + q)], ["yko%d" % q], T.yko[0:8, 448 * q:448 * q + 448], T["B%d" % (4 + q)][0:8, 0:448])
                 dma("y", ["yko%d" % q for q in range(4)], [], "outs", T.yk[:], T.yko[0:8, :])
             else:
                 kin_lines()

from concourse.mybir import dt, AluOpType as OP, AxisListType as AX, ActivationFunctionType as AF

V, P, T9, W = 1792, 256, 9, 2048
BIG = float(1 << 20)
MAGIC = 1.5 * (1 << 23) * 64
KV = 11
CHUNKS = [(0, 4), (4, 4), (8, 4), (12, 4)]
MA = (5, 6)
GRAM = [[("B3", "v", (7, 6, 5, 4, 1, 0))], [("B7", "s", (15, 14)), ("B5", "v", (11, 10, 3, 2)), ("B0", "s", (13,)), ("B4", "v", (12, 9, 8))]]
SEG, BASE = {}, {}
_o = 0
for _b, _q, _aa in GRAM[0] + GRAM[1]:
    if _q == "v":
        BASE[_b] = _o
        for _a in _aa:
            SEG[_a] = (_o, _o + 16 * _a + 15)
            _o += 16 * _a + 16
NSC = _o
SA = [_a for _a in range(16) if _a not in SEG]

F32, BF16, F16, I32, U16 = "float32", "bfloat16", "float16", "int32", "uint16"
SCRATCH = {"B%d" % i: ("psum", [128, 512], F32) for i in range(8)}
for _n, _s, _d in [
        ("X", [W], F32), ("K", [W], F32), ("HE", [W], F32), ("IDT", [W], F32), ("IND", [W], BF16), ("BT", [3584], BF16),
        ("kinb", [V], I32), ("xb", [V], BF16), ("ownb", [16], I32), ("holdb", [16], I32), ("wallb", [16], I32), ("wtb", [1], I32), ("prb", [P], BF16),
        ("Yl", [9, P], BF16), ("Yo", [9, P], BF16), ("El", [9, 16], U16), ("Eo", [9, 16], U16), ("Hl", [9, 16], U16), ("Ho", [9, 16], U16),
        ("Wo", [16], U16), ("W1", [16], U16), ("W2", [16], U16),
        ("yexp", [16 * P], BF16), ("cU", [P], U16), ("c16", [P], F16), ("Em", [16, 32], F16), ("cm", [P], F32),
        ("DL", [16 * P], F16), ("AB", [16, P], F16), ("s64", [P], F32), ("mm", [P], F32), ("key", [P], F32),
        ("ks", [P], F32), ("RST", [128], F32), ("keyi", [32], I32), ("BE", [32], I32), ("FE", [16], F32), ("DJ2", [32], F32), ("A0", [32], F32), ("A12", [32], F32),
        ("dk", [16], U16), ("bu", [16], U16), ("e17", [16], F32), ("VB", [1], F32), ("uB", [16], F32), ("hx", [16], F32),
        ("C", [P], BF16), ("BDC", [16, 128], BF16), ("D", [32], F32), ("junk", [16, P], BF16), ("nd", [32], F32), ("o12", [32], U16),
        ("SC", [NSC + 16], F32), ("RSTG", [NSC], F32), ("ENDS", [16], F32), ("ENDM", [16], F32), ("ENDC", [1], F32), ("ENDL", [2], U16), ("BIAS2", [32], F32),
        ("M3", [64], F16), ("OHS", [16], F16),
        ("fr", [P], F32), ("KF", [P], F32), ("yqa", [P], F32), ("yqr", [P], F32), ("yq", [P], BF16), ("xg", [P], BF16), ("diff", [P], F32), ("red", [P], BF16), ("IDB", [128], BF16), ("NIB", [128], BF16),
        ("em", [P], F32), ("es", [P], F32), ("NZ", [P], F32), ("e1n", [16], F32),
        ("hn", [16], F32), ("hw", [16], F32), ("wf", [16], F32), ("nw", [16], F32),
        ("ti", [P], I32), ("ti2", [P], I32), ("si", [16], I32), ("si2", [16], I32), ("si3", [16], F32),
        ("pidx", [1], I32), ("cols", [32], F32), ("ints", [8], I32), ("i8", [8], F32), ("GM", [8], F32), ("m1", [8], F32), ("m2", [8], F32),
        ("k16", [P], F32), ("DELTA", [P], F32), ("OH", [16], F16), ("SEL", [16, 128], F16), ("SELW", [16, 128], BF16), ("IDN", [128], F16), ("KKC", [P], F16),
        ("i128", [128], F32), ("POS", [P], F32), ("PJ", [32], F32), ("BIAS", [16], F32), ("DJ", [16], F32), ("ONES", [P], F32),
        ("WI", [520], F32), ("WB", [520], I32), ("WC", [520], I32), ("LOWC", [512], BF16), ("HIGH", [8], F32), ("KW", [8], F16),
        ("K16", [V], F16), ("yxo", [V], BF16), ("yko", [V], F32), ("ro", [2, P], F32)]:
    SCRATCH[_n] = ("sbuf", [128] + _s, _d)
SEMAPHORES = ["v", "s", "p", "g", "lsem", "w1", "w2", "outs"] + ["ld%d" % i for i in range(7)] + [a + str(t) for a in "yeh" for t in range(1, T9)]


def rank_program(g, core, T, topo):
    rank = T.rank_of(core)
    if rank is None:
        return
    n = len(T.cores)
    eng = {"v": g.vector, "s": g.scalar, "p": g.tensor, "g": g, "y": g.sync}
    cnt = {}
    known = {q: {} for q in eng}
    snap = {}
    wr, rd = {}, {}

    def need(q, ev):
        _, sem, val = ev
        if known[q].get(sem, 0) < val:
            eng[q].wait_ge(T.sem[sem], val)
            for s2, v2 in list(snap.get((sem, val), {}).items()) + [(sem, val)]:
                if known[q].get(s2, 0) < v2:
                    known[q][s2] = v2

    def before(q, r, w):
        evs = []
        for k in r:
            if k in wr:
                evs.append(wr[k])
        for k in w:
            if k in wr:
                evs.append(wr[k])
            for e in rd.get(k, []):
                if e[0] != q:
                    evs.append(e)
        best = {}
        for e in evs:
            if e[1] not in best or best[e[1]][2] < e[2]:
                best[e[1]] = e
        for e in sorted(best.values(), key=lambda e: -e[2]):
            need(q, e)

    def after(ev, r, w):
        for k in r:
            rd.setdefault(k, []).append(ev)
        for k in w:
            wr[k] = ev
            rd[k] = []

    def op(q, r, w, fn):
        before(q, r, w)
        i = fn(eng[q])
        cnt[q] = cnt.get(q, 0) + 1
        i.then_inc(T.sem[q], 1)
        ev = (q, q, cnt[q])
        snap[(q, cnt[q])] = dict(known[q])
        after(ev, r, w)

    def dma(q, r, w, sem, out, in_):
        before(q, r, w)
        eng[q].dma_start(out, in_).then_inc(T.sem[sem], 16)
        cnt[sem] = cnt.get(sem, 0) + 16
        snap[(sem, cnt[sem])] = dict(known[q])
        after(("dma", sem, cnt[sem]), r, w)

    def send(dst, r, out, in_, sem):
        before("g", r, [])
        rid, pid = topo.addr(dst, core)
        m = topo.mask(core, dst)
        g.remote_dma(out, in_, T.sem[sem], T.sem.lsem, pid, rid, m)
        cnt["lsem"] = cnt.get("lsem", 0) + len(topo.engines(core, dst))

    def landing(src, w, sem):
        val = len(topo.engines(src, core))
        for k in w:
            wr[k] = ("remote", sem, val)
            rd[k] = []

    def ts(q, r, w, out, in0, s1, s2, o0, o1=None):
        if o1 is None:
            op(q, r, w, lambda e: e.tensor_scalar(out, in0, s1, None, o0))
        else:
            op(q, r, w, lambda e: e.tensor_scalar(out, in0, s1, s2, o0, o1))

    def tt(r, w, out, in0, in1, o):
        op("v", r, w, lambda e: e.tensor_tensor(out, in0, in1, o))

    def cp(r, w, out, in_):
        op("v", r, w, lambda e: e.tensor_copy(out, in_))

    def act(r, w, out, in_, f, **kw):
        op("s", r, w, lambda e: e.activation(out, in_, f, **kw))

    def fill(w, ap, c):
        op("v", [], w, lambda e: e.memset(ap, c))

    nxt, prv = T.cores[(rank + 1) % n], T.cores[(rank - 1) % n]
    nx2, pv2 = T.cores[(rank + 2) % n], T.cores[(rank - 2) % n]

    dma("y", [], ["ownb"], "ld0", T.ownb[:], T.own[:])
    dma("y", [], ["kinb"], "ld1", T.kinb[:], T.kin[:])
    dma("s", [], ["prb"], "ld2", T.prb[:], T.price[:])
    dma("s", [], ["xb"], "ld3", T.xb[:], T.x[:])
    dma("y", [], ["wallb"], "ld4", T.wallb[:], T.wall[:])
    dma("y", [], ["holdb"], "ld5", T.holdb[:], T.hold[:])
    dma("y", [], ["wtb"], "ld6", T.wtb[:], T.wt[:])

    def iota(k, out, pat, base, cm, f=True):
        op("g", [], [k], lambda e: e.iota(out, pat, base, cm, allow_small_or_imprecise_dtypes=f))
    iota("pidx", T.pidx[:], [[0, 1]], 0, 1, False)
    iota("i8", T.i8[:], [[1, 8]], 0, 0)
    iota("k16", T.k16[:], [[0, 16], [1, 16]], 0, 0)
    iota("WI", T.WI[:, 0:512], [[1, 512]], 0, 0)
    iota("WI2", T.WI[:, 512:520], [[512, 8]], 0, 0)
    iota("PJ", T.PJ[:], [[0, 2], [16, 16]], 0, 0)
    iota("i128", T.i128[:], [[1, 128]], 0, 0)
    iota("POS", T.POS[:], [[1, P]], 0, 0)
    iota("Xt", T.X[:, V:W], [[0, W - V]], 1, 0)
    iota("Kt", T.K[:, V:W], [[0, W - V]], 0, 0)
    iota("ONES", T.ONES[:], [[0, P]], 1, 0)
    iota("RSTG", T.RSTG[:], [[0, NSC]], (1 << 24) - 1, 0)
    iota("SC", T.SC[:, NSC:NSC + 16], [[0, 16]], 0, 0)
    for a in range(16):
        iota("ENDS%d" % a, T.ENDS[:, a:a + 1], [[0, 1]], SEG[a][1] if a in SEG else NSC + a, 0)
        if a in SEG:
            iota("RSTG", T.RSTG[:, SEG[a][0]:SEG[a][0] + 1], [[0, 1]], 1 - (1 << 24), 0)
    iota("IDT", T.IDT[:], [[1, W]], 0, 0)
    iota("HE", T.HE[:], [[1, W]], 0, 0)

    col = {}

    def c_(name):
        col.setdefault(name, len(col))
        i = col[name]
        return T.cols[:, i:i + 1]
    ii, gi = T.ints[:, 0:1], T.ints[:, 1:2]
    ts("v", ["pidx"], ["ii"], ii, T.pidx[:], 15, None, OP.bitwise_and)
    ts("v", ["pidx"], ["gi"], gi, T.pidx[:], 4, None, OP.logical_shift_right)
    cp(["pidx"], ["pF"], c_("pF"), T.pidx[:])
    cp(["ii"], ["iF"], c_("iF"), ii)
    cp(["gi"], ["gF"], c_("gF"), gi)
    for b in range(4):
        ts("v", ["ii"], ["ib%d" % b], T.ints[:, 2 + b:3 + b], ii, b, 1, OP.logical_shift_right, OP.bitwise_and)
    ts("v", ["gi"], ["gb"], T.ints[:, 6:7], gi, 1, None, OP.bitwise_and)
    for b in range(4):
        ts("v", ["ib%d" % b], ["pb%d" % b], c_("pb%d" % b), T.ints[:, 2 + b:3 + b], 2.0 ** -(1 << b) - 1.0, 1.0, OP.mult, OP.add)
    cp(["ib0"], ["odd"], c_("odd"), T.ints[:, 2:3])
    ts("v", ["ib0"], ["even"], c_("even"), T.ints[:, 2:3], -1.0, 1.0, OP.mult, OP.add)
    cp(["gb"], ["gO"], c_("gO"), T.ints[:, 6:7])
    ts("v", ["gb"], ["gE"], c_("gE"), T.ints[:, 6:7], -1.0, 1.0, OP.mult, OP.add)
    tt(["pb0", "pb1"], ["pa"], c_("pa"), c_("pb0"), c_("pb1"), OP.mult)
    tt(["pb2", "pb3"], ["pc"], c_("pc"), c_("pb2"), c_("pb3"), OP.mult)
    ts("v", ["iF"], ["l9"], c_("l9"), c_("iF"), 9.0, None, OP.is_lt)
    ts("v", ["iF"], ["l12"], c_("l12"), c_("iF"), 12.0, None, OP.is_lt)
    ts("v", ["iF"], ["b12"], c_("b12"), c_("iF"), 12.0, BIG, OP.is_equal, OP.mult)
    ts("v", ["iF"], ["q12"], c_("q12"), c_("iF"), 12.0, -1.0 / 256, OP.is_equal, OP.mult)
    tt(["pa", "pc"], ["pw"], c_("pw"), c_("pa"), c_("pc"), OP.mult)
    ts("v", ["l12"], ["s12"], c_("s12"), c_("l12"), BIG, None, OP.mult)
    ts("v", ["l9"], ["l9d"], c_("l9d"), c_("l9"), 2.0, None, OP.mult)
    ts("v", ["l9"], ["l9n"], c_("l9n"), c_("l9"), -1.0, None, OP.mult)
    tt(["l12", "l9"], ["h3"], c_("h3"), c_("l12"), c_("l9"), OP.subtract)
    ts("v", ["iF"], ["i1"], c_("i1"), c_("iF"), 1.0, None, OP.add)
    ts("v", ["pw"], ["ph"], c_("ph"), c_("pw"), 0.5, -0.5, OP.mult, OP.add)
    ts("v", ["h3"], ["h3d"], c_("h3d"), c_("h3"), 2.0, None, OP.mult)
    ts("v", ["h3"], ["h3n"], c_("h3n"), c_("h3"), -1.0, None, OP.mult)
    ts("v", ["i8", "gF"], ["GM"], T.GM[:], T.i8[:], c_("gF"), None, OP.is_equal)
    ts("v", ["k16", "iF"], ["OH"], T.OH[:], T.k16[:, 0:16], c_("iF"), None, OP.is_equal)
    ts("v", ["k16", "iF"], ["DELTA"], T.DELTA[:], T.k16[:], c_("iF"), None, OP.is_equal)
    ts("v", ["k16"], ["KKC"], T.KKC[:], T.k16[:], 2.0, -32.0, OP.mult, OP.add)
    ts("v", ["i128", "pF"], ["IDN"], T.IDN[:], T.i128[:], c_("pF"), None, OP.is_equal)
    sel = ["SEL%d" % r for r in range(16)]
    fill(sel, T.SEL[:], 0.0)
    for r in range(16):
        if r < 8:
            cp(["GM"], ["SEL%d" % r], T.SEL[:, r, r:128:16], T.GM[:])
        else:
            act(["GM"], ["SEL%d" % r], T.SEL[:, r, r:128:16], T.GM[:], AF.Copy)
    fill(["M3"], T.M3[:], -3.0)
    ts("v", ["OH"], ["OHS"], T.OHS[:], T.OH[:], 1.0 / 512, None, OP.mult)
    ts("v", ["WI", "pw", "ph"], ["WB"], T.WB[:, 0:512], T.WI[:, 0:512], c_("pw"), c_("ph"), OP.mult, OP.add)
    ts("v", ["WI2", "pw", "ph"], ["WB2"], T.WB[:, 512:520], T.WI[:, 512:520], c_("pw"), c_("ph"), OP.mult, OP.add)
    ts("v", ["WB", "WB2"], ["WC"], T.WC[:], T.WB[:], 1, None, OP.bitwise_and)
    ts("v", ["WC", "l9d", "l9n"], ["LOWC"], T.LOWC[:], T.WC[:, 0:512], c_("l9d"), c_("l9n"), OP.mult, OP.add)
    ts("v", ["WC", "h3d", "h3n"], ["HIGH"], T.HIGH[:], T.WC[:, 512:520], c_("h3d"), c_("h3n"), OP.mult, OP.add)

    cp(["ownb"], ["El0"], T.El[:, 0, :], T.ownb[:])
    ts("v", ["prb"], ["Yl0"], T.Yl[:, 0, :], T.prb[:], 64.0, None, OP.mult)
    ts("v", ["xb"], ["Xa"], T.X[:, 0:768], T.xb[:, 0:768], 64.0, 1.0, OP.mult, OP.add)
    act(["xb"], ["Xb"], T.X[:, 768:V], T.xb[:, 768:V], AF.Copy, scale=64.0, bias=1.0)
    XK, KK = ["Xa", "Xb", "Xt"], ["K", "Kt"]
    cp(["wallb"], ["Wo"], T.Wo[:], T.wallb[:])
    send(nxt, ["Wo"], T.W1[:], T.Wo[:], "w1")
    send(nx2, ["Wo"], T.W2[:], T.Wo[:], "w2")
    landing(prv, ["W1"], "w1")
    landing(pv2, ["W2"], "w2")
    cp(["holdb"], ["Hl0"], T.Hl[:, 0, :], T.holdb[:])

    def late_constants():
        for u in range(7):
            o = T.BT[:, 512 * u:512 * u + 512]
            if u < 5:
                ts("v", ["LOWC", "HIGH"], ["BT%d" % u], o, T.LOWC[:], T.HIGH[:, u:u + 1], None, OP.add)
            else:
                act(["LOWC", "HIGH"], ["BT%d" % u], o, T.LOWC[:], AF.Identity, bias=T.HIGH[:, u:u + 1])
        act(["kinb"], ["K"], T.K[:, 0:V], T.kinb[:], AF.Copy)
        ts("v", ["POS", "q12"], ["POS"], T.POS[:], T.POS[:], c_("q12"), None, OP.mult)
        ts("v", ["GM", "s12"], ["m1"], T.m1[:], T.GM[:], c_("s12"), None, OP.mult)
        ts("v", ["GM", "b12"], ["m2"], T.m2[:], T.GM[:], c_("b12"), None, OP.mult)
        ts("v", ["GM", "i1"], ["KW"], T.KW[:], T.GM[:], c_("i1"), None, OP.mult)
        ts("v", ["PJ", "iF"], ["PJ"], T.PJ[:], T.PJ[:], c_("iF"), None, OP.add)
        ts("v", ["PJ"], ["BIAS"], T.BIAS[:], T.PJ[:, 0:16], BIG / 256, -12.0 * BIG, OP.mult, OP.add)
        ts("v", ["PJ"], ["DJ2"], T.DJ2[:], T.PJ[:], float(V), None, OP.add)
        ts("v", ["PJ"], ["BIAS2"], T.BIAS2[:], T.PJ[:], BIG / 256, -12.0 * BIG, OP.mult, OP.add)
        for a in SA:
            fill(["BIAS2"], T.BIAS2[:, a:32:16], 0.0)
        tt(["OH"] + ["ENDS%d" % a for a in range(16)], ["ENDM"], T.ENDM[:], T.ENDS[:], T.OH[:], OP.mult)
        op("v", ["ENDM"], ["ENDC"], lambda e: e.tensor_reduce(T.ENDC[:], T.ENDM[:], AX.X, OP.add))
        for i in range(2):
            cp(["ENDC"], ["ENDL%d" % i], T.ENDL[:, i:i + 1], T.ENDC[:])
        fill(["INDa"], T.IND[:, 0:V], 64.0)
        fill(["INDb"], T.IND[:, V:W], 0.0)
        ts("v", ["k16"], ["RST"], T.RST[:], T.k16[:, 0:128], 0.0, float(1 << 26), OP.is_equal, OP.mult)
        ts("v", ["RST"], ["RST"], T.RST[:], T.RST[:], -float(1 << 25), None, OP.add)
        ts("v", ["k16"], ["NZ"], T.NZ[:], T.k16[:], 0.0, None, OP.is_gt)
        cp(["IDN"], ["IDB"], T.IDB[:], T.IDN[:])
        ts("v", ["IDN"], ["NIB"], T.NIB[:], T.IDN[:], -1.0, None, OP.mult)
        fill(["VB"], T.VB[:], 4096.0 * V)

    def closing_kin():
        dma("y", ["HE"], [], "outs", T.yh[:], T.HE[0:128:16, 0:V])
        for q in range(4):
            s, bk = slice(448 * q, 448 * q + 448), "B%d" % (4 + q)
            act(KK, ["K16_%d" % q], T.K16[:, s], T.K[:, s], AF.Copy)
            op("p", ["K16_%d" % q, "KW"], [bk], lambda e: e.matmul(T[bk][0:8, 0:448], T.KW[:], T.K16[:, s], True, True))
        act(XK, ["yxo"], T.yxo[:], T.X[:, 0:V], AF.Copy, scale=1.0 / 64, bias=-1.0 / 64)
        dma("y", ["yxo"], [], "outs", T.yx[:], T.yxo[:])
        for q in range(2):
            s, bk = slice(448 * q, 448 * q + 448), "B%d" % (4 + q)
            act([bk], ["yko%d" % q], T.yko[0:8, s], T[bk][0:8, 0:448], AF.Copy)

    for t in range(T9):
        jub, last = t % 3 == 2, t == T9 - 1
        Yt, Et, Ht = "Yl%d" % t, "El%d" % t, "Hl%d" % t
        if t:
            landing(prv, [Yt], "y%d" % t)
            landing(prv, [Et], "e%d" % t)
            landing(prv, [Ht], "h%d" % t)
        yv, eu, hv = T.Yl[:, t, :], T.El[:, t, :], T.Hl[:, t, :]
        yx = ["yx%d" % k for k in range(16)]
        for k in range(16):
            if k < KV:
                cp([Yt], ["yx%d" % k], T.yexp[:, k:16 * P:16], yv)
            else:
                act([Yt], ["yx%d" % k], T.yexp[:, k:16 * P:16], yv, AF.Copy)
        kt, kk = (T.K, KK) if t else (T.kinb, ["kinb"])
        cp(kk + [Et], ["cU"], T.cU[:], kt[:].indirect(eu))
        act(kk + [Et], ["c16"], T.c16[:], kt[:].indirect(eu), AF.Copy)
        act(["c16", "gE"], ["Em0"], T.Em[:, :, 0:16], T.c16[:], AF.Copy, scale=c_("gE"))
        act(["c16", "gO"], ["Em1"], T.Em[:, :, 16:32], T.c16[:], AF.Copy, scale=c_("gO"))
        act([Et], ["e17"], T.e17[:], eu, AF.Copy, bias=float(V))
        act([Et], ["BEe"], T.BE[:, 16:32], eu, AF.Copy)
        act(["c16", "even"], ["cm"], T.cm[:], T.c16[:], AF.Copy, scale=c_("even"))

        def kc(e):
            e.matmul(T.B2[:, 0:P], T.IDN[:], T.KKC[:], True, False)
            for A in range(4):
                s = slice(32 * A, 32 * A + 32)
                for a in range(16):
                    e.matmul(T.B2[s, 16 * a:16 * a + 16], T.Em[s, a, :], T.OHS[s, :], False, False)
            return e.matmul(T.B2[:, 0:P], T.IDN[:], T.KKC[:], False, True)
        op("p", ["Em0", "Em1", "OHS", "IDN", "KKC"], ["B2"], kc)
        for ch, (a0, na) in enumerate(CHUNKS):
            s, f = slice(a0, a0 + na), slice(256 * a0, 256 * (a0 + na))
            tt(XK + ["cU"] + yx, ["DL%d" % ch], T.DL[:, f], T.X[:].indirect(T.cU[:, 16 * a0:16 * (a0 + na)]), T.yexp[:, f], OP.subtract)
            act(["DL%d" % ch], ["AB%d" % ch], T.AB[:, s, :], T.DL[:, f], AF.Abs)
            zb, o = ("B0", "B1")[a0 // 8], 16 * (a0 % 8)

            def zsum(e):
                e.matmul(T[zb][:, o:o + 16 * na], T.IDN[:], T.M3[:, 0:16 * na], True, False)
                for r in range(16):
                    i = e.matmul(T[zb][:, o:o + 16 * na], T.SEL[:, r, :], T.AB[:, s, 16 * r:16 * r + 16], False, r == 15)
                return i
            op("p", ["AB%d" % ch, "M3", "IDN"] + sel, [zb], zsum)
        if t == 0:
            late_constants()

        def quarter():
            act([Yt], ["yqa"], T.yqa[:], yv, AF.Copy, scale=0.25, bias=-24.0)
            act(["yqa"], ["yqr"], T.yqr[:], T.yqa[:], AF.Copy, bias=MAGIC)
            act(["yqr"], ["yq"], T.yq[:], T.yqr[:], AF.Copy, bias=-MAGIC)
        if jub:
            wl, wk = ((T.W2, "W2"), (T.W1, "W1"), (T.Wo, "Wo"))[t // 3]
            act([wk], ["wf"], T.wf[:], wl[:], AF.Copy)
            act([wk], ["nw"], T.nw[:], wl[:], AF.Copy, scale=-1.0, bias=1.0)
        for h in range(2):
            zb, s, x = ("B0", "B1")[h], slice(8 * h, 8 * h + 8), str(h)
            z = T[zb][:, 0:128]
            sb = ("B4", "B5")[h]
            poor, m = T[sb][:, 0:128], slice(128 * h, 128 * h + 128)
            ts("v", [zb], ["s64" + x], T.s64[:, m], z, MAGIC, -MAGIC, OP.add, OP.add)
            tt([zb, "s64" + x], [sb], poor, z, T.s64[:, m], OP.is_lt)
            tt([sb, "s64" + x], ["mm" + x], T.mm[:, m], T.s64[:, m], poor, OP.mult)
            tt(["mm" + x, "B2"], ["key" + x], T.key[:, m], T.mm[:, m], T.B2[:, 128 * h:128 * h + 128], OP.add)
            op("v", ["key" + x, "RST"], ["ks" + x], lambda e: e.tensor_tensor_scan(T.ks[:, m], T.RST[:], T.key[:, m], 0.0, OP.max, OP.min))
            ts("v", ["ks" + x], ["keyi" + x], T.keyi[:, s], T.ks[:, 128 * h + 15:128 * h + 128:16], 512.0, None, OP.mult)
            ts("v", ["keyi" + x], ["bi" + x], T.BE[:, s], T.keyi[:, s], 2047, None, OP.bitwise_and)
            tt(["keyi" + x, "e17"], ["FE" + x], T.FE[:, s], T.keyi[:, s], T.e17[:, s], OP.min)
            act(["bi" + x], ["bu" + x], T.bu[:, s], T.BE[:, s], AF.Copy)
            if h:
                act(["keyi0", "keyi1"], ["nk"], T.keyi[:, 16:32], T.keyi[:, 0:16], AF.Copy, scale=-8.0)
            tt(["bi" + x, "FE" + x], ["dk" + x], T.dk[:, s], T.BE[:, s], T.FE[:, s], OP.max)
            tt(["BT%d" % u for u in range(7)] + ["dk" + x, "POS"], ["C" + x], T.C[:, m], T.BT[:].indirect(T.dk[:, s]), T.POS[:, m], OP.add)
            for q in range(8):
                if q < MA[h]:
                    ts("v", ["C" + x, "m1", "m2"], ["BD%d_%d" % (h, q)], T.BDC[:, s, 16 * q:16 * q + 16], T.C[:, m], T.m1[:, q:q + 1], T.m2[:, q:q + 1], OP.mult, OP.add)
                else:
                    act(["C" + x, "m1", "m2"], ["BD%d_%d" % (h, q)], T.BDC[:, s, 16 * q:16 * q + 16], T.C[:, m], AF.Identity, scale=T.m1[:, q:q + 1], bias=T.m2[:, q:q + 1])
            for bank, _, aa in GRAM[h]:
                def gram(e):
                    o = 0
                    for a in aa:
                        i = e.matmul(T[bank][:, o:o + 16 * a + 16], T.BDC[:, a, :], T.C[:, 0:16 * a + 16], True, True)
                        o += 16 * a + 16
                    return i
                op("p", ["C0", "C" + x] + ["BD%d_%d" % (h, q) for q in range(8)], [bank], gram)
            if h == 0 and jub:
                quarter()
            if h:
                act(["IDT", "bu0", "bu1"], ["fr"], T.fr[:], T.IDT[:].indirect(T.bu[:]), AF.Copy)
        bus = ["bu0", "bu1"]
        tt(["keyi0", "keyi1", "nk", "DJ2"], ["A0"], T.A0[:], T.keyi[:], T.DJ2[:], OP.min)
        tt(["A0", "bi0", "bi1", "BEe"], ["A12"], T.A12[:], T.A0[:], T.BE[:], OP.max)
        for bank, q, aa in GRAM[0] + GRAM[1]:
            o, w = 0, sum(16 * a + 16 for a in aa)
            if q == "v":
                z, b = T[bank][:, 0:w], BASE[bank]
                op("v", [bank, "RSTG", "SC"], ["SC" + bank], lambda e: e.tensor_tensor_scan(T.SC[:, b:b + w], T.RSTG[:, b:b + w], z, 0.0, OP.min, OP.max))
                continue
            for a in aa:
                z = T[bank][:, o:o + 16 * a + 16]
                o += 16 * a + 16
                act([bank, "BIAS", "SC"], ["SC%d" % a, "junk%d" % a], T.junk[:, a, 0:16 * a + 16], z, AF.Relu, bias=T.BIAS[:, a:a + 1], accum_out=T.SC[:, NSC + a:NSC + a + 1])
        tt(["SC"] + ["SC" + b for b in BASE] + ["SC%d" % a for a in SA] + ["ENDL0", "ENDL1", "BIAS2"], ["D"], T.D[:], T.SC[:].indirect(T.ENDL[:]), T.BIAS2[:], OP.add)
        tt(["D", "DJ2"], ["nd"], T.nd[:], T.D[:], T.DJ2[:], OP.min)
        tt(["nd", "A12"], ["o1", "o2"], T.o12[:], T.A12[:], T.nd[:], OP.max)
        o1, o2 = T.o12[:, 0:16], T.o12[:, 16:32]

        def redeem_wealth():
            tt(["diff", "o1", "ONES"], XK, T.X[:].indirect(o1), T.diff[:], T.ONES[:], OP.add)

        def kin_lines():
            tt(["KF", "cm", "o2"], KK, T.K[:].indirect(o2), T.KF[:], T.cm[:], OP.add)

        def holders():
            tt(["uB", Ht], ["hx"], T.hx[:], T.uB[:], hv, OP.max)
        def kin_of_kin():
            act(kk + ["bu0", "bu1", "odd"], ["KF"], T.KF[:], kt[:].indirect(T.bu[:]), AF.Copy, scale=c_("odd"))

        def wealth_of_kin():
            act(XK + bus, ["xg"], T.xg[:], T.X[:].indirect(T.bu[:]), AF.Copy, bias=-1.0)

        def paid():
            op("p", ["IDB", "NIB", "yq", "xg"], ["B6"], lambda e: (e.matmul(T.B6[:, 0:P], T.IDB[:], T.xg[:], True, False), e.matmul(T.B6[:, 0:P], T.NIB[:], T.yq[:], False, True))[1])
            act(["B6"], ["diff"], T.diff[:], T.B6[:, 0:P], AF.Relu)

        def raised():
            act(["INDa", "INDb", "o1"], ["red"], T.red[:], T.IND[:].indirect(o1), AF.Copy)
            op("p", ["IDB", "red"], ["B2"], lambda e: e.matmul(T.B2[:, 0:P], T.IDB[:], T.red[:], False, True))
        op("p", ["IDB", Yt], ["B2"], lambda e: e.matmul(T.B2[:, 0:P], T.IDB[:], yv, True, False))
        if jub:
            wealth_of_kin()
            paid()
            raised()
            act(["o1"], ["uB"], T.uB[:], o1, AF.Relu, scale=-4096.0, bias=T.VB[:])
            kin_of_kin()
        else:
            kin_of_kin()
            raised()
            act(["o1"], ["uB"], T.uB[:], o1, AF.Relu, scale=-4096.0, bias=T.VB[:])
            wealth_of_kin()
            quarter()
            paid()

        cp(["fr", "o2"], ["HE"], T.HE[:].indirect(o2), T.fr[:])
        Yk, Ek, Hk = "Yo%d" % t, "Eo%d" % t, "Ho%d" % t
        yo, eo, ho = T.Yo[:, t, :], T.Eo[:, t, :], T.Ho[:, t, :]
        if not jub:
            ts("v", ["B2"], [Yk], yo, T.B2[:, 0:P], 960.0, None, OP.min)
            send(nxt, [Yk], T.Yl[:, t + 1, :], yo, "y%d" % (t + 1))
        else:
            redeem_wealth()
            ts("v", ["B2"], ["y1"], T.prb[:], T.B2[:, 0:P], 960.0, None, OP.min)
            if last:
                kin_lines()
                closing_kin()
            holders()
            tt(["hx", "o1"], ["hn"], T.hn[:], T.hx[:], o1, OP.min)
            tt(["hn", "wf"], ["hw"], T.hw[:], T.hn[:], T.wf[:], OP.mult)
        tt(["HE", Et, "DELTA"], ["em"], T.em[:], T.HE[:].indirect(eu), T.DELTA[:], OP.mult)
        op("v", ["em", "NZ"], ["es"], lambda e: e.tensor_tensor_scan(T.es[:], T.NZ[:], T.em[:], 0.0, OP.mult, OP.add))
        if not jub:
            cp(["es"], [Ek], eo, T.es[:, 15:P:16])
            send(nxt, [Ek], T.El[:, t + 1, :], eo, "e%d" % (t + 1))
            kin_lines()
            redeem_wealth()
            holders()
            tt(["hx", "o1"], [Hk], ho, T.hx[:], o1, OP.min)
            send(nxt, [Hk], T.Hl[:, t + 1, :], ho, "h%d" % (t + 1))
        else:
            tt(["es", "nw"], ["e1n"], T.e1n[:], T.es[:, 15:P:16], T.nw[:], OP.mult)
            tt(["e1n", "hw"], [Ek], eo, T.e1n[:], T.hw[:], OP.max)
            if not last:
                send(nxt, [Ek], T.El[:, t + 1, :], eo, "e%d" % (t + 1))
            tt(XK + [Ek, "y1"], ["ti"], T.ti[:], T.X[:].indirect(eo), T.prb[:], OP.add)
            ts("v", ["ti"], ["ti2"], T.ti2[:], T.ti[:], 7, None, OP.arith_shift_right)
            ts("v", ["ti2"], [Yk], yo, T.ti2[:], 64.0, None, OP.mult)
            if not last:
                send(nxt, [Yk], T.Yl[:, t + 1, :], yo, "y%d" % (t + 1))
            if t == 2:
                cp(["wtb"], ["wtF"], c_("wtF"), T.wtb[:])
                ts("v", sel + ["wtF"], ["SELW"], T.SELW[:], T.SEL[:], c_("wtF"), None, OP.mult)

            def wsum(e):
                for r in range(16):
                    i = e.matmul(T.B2[:, 0:16], T.SELW[:, r, :], T.Yo[:, t, r:P:16], r == 0, r == 15)
                return i
            op("p", ["SELW", Yk], ["B2"], wsum)
            if last:
                cp(["IDT", Ek], ["ro0"], T.ro[:, 0, :], T.IDT[:].indirect(eo))
                dma("y", ["ro0"], [], "outs", T.yo[:], T.ro[0:128:16, 0, :])
                for q in range(2, 4):
                    cp(["B%d" % (4 + q)], ["yko%d" % q], T.yko[0:8, 448 * q:448 * q + 448], T["B%d" % (4 + q)][0:8, 0:448])
                dma("y", ["yko%d" % q for q in range(4)], [], "outs", T.yk[:], T.yko[0:8, :])
            else:
                kin_lines()
            cp(["B2"], ["si"], T.si[:], T.B2[:, 0:16])
            ts("v", ["si"], ["si2"], T.si2[:], T.si[:], 6, 2047, OP.logical_shift_right, OP.bitwise_and)
            ts("v", ["si2"], ["si3"], T.si3[:], T.si2[:], float(V), -float(V), OP.is_ge, OP.mult)
            tt(["si2", "si3"], [Hk], ho, T.si2[:], T.si3[:], OP.add)
            if not last:
                send(nxt, [Hk], T.Hl[:, t + 1, :], ho, "h%d" % (t + 1))

    cp(["IDT", "Ho8"], ["ro1"], T.ro[:, 1, :], T.IDT[:].indirect(T.Ho[:, 8, :]))
    dma("y", ["ro1"], [], "outs", T.yt[:], T.ro[0:128:16, 1, :])
    for sem in ("v", "s", "p", "g", "lsem", "outs"):
        g.wait_ge(T.sem[sem], cnt[sem])
